import numpy as np, ml_dtypes
CORES = [24,25,26,27,28,29,30,31]
N = 8
import mx_ref
BF = ml_dtypes.bfloat16
def cols(t, e):
    v = np.concatenate([t.reshape(128, -1, 4), np.zeros((128, 1, 4), BF)], axis=1)
    return np.ascontiguousarray(v[:, e]).reshape(128, -1)
def cut(t, i, w=512):
    return t[:, w * i:w * i + w]
def tile(rs):
    return np.stack(rs, axis=2).reshape(128, -1).astype(BF)
def pick(q, e):
    c = np.concatenate([q[0].reshape(128, -1, 4), np.zeros((128, 1, 4), np.uint8)], axis=1); s = np.concatenate([q[1], np.ones((16, 1), np.uint8)], axis=1)
    return (np.ascontiguousarray(c[:, e].reshape(128, -1)), np.ascontiguousarray(s[:, e]))
def join(*qs):
    return (np.concatenate([q[0] for q in qs], axis=1), np.concatenate([q[1] for q in qs], axis=1))
def put(q, e, v):
    c, s = q[0].reshape(128, -1, 4).copy(), q[1].copy(); c[:, e] = v[0].reshape(128, -1, 4); s[:, e] = v[1]
    return (c.reshape(128, -1), s)
def pk(c, s):
    return (np.ascontiguousarray(c), mx_ref.live(s))
def emit(q):
    return q[0], q[1]
def decode(q):
    o = []
    for b in range(4):
        e = np.zeros((128, 128, 4), np.float32); e[np.arange(128), np.arange(128), b] = 1
        o.append(mx_ref.matmul(mx_ref.quantize(e.reshape(128, 512).astype(BF)), q))
    return np.stack(o, axis=2).reshape(128, -1)
def f(rng, *shape):
    return mx_ref.flush((rng.standard_normal(shape, dtype=np.float32) * np.exp2(rng.integers(-2, 3, shape[:-1] + (1,)))).astype(BF))
def wide(rng, *shape, cols=0):
    v = rng.standard_normal(shape, dtype=np.float32) * np.exp2(rng.integers(-12, 13, shape)).astype(np.float32)
    if cols: v *= np.repeat(np.exp2(rng.integers(-cols, cols + 1, shape[:-2] + (1, shape[-1] // 4))) * (rng.random(shape[:-2] + (1, shape[-1] // 4)) > 0.0625), 4, axis=-1).astype(np.float32)
    return mx_ref.flush(v.astype(BF))
T, CAPP, CAPR = 128, 48, 16
def big(v, k):
    v = v.astype(np.float32) * np.float32(k)
    v[np.abs(v) < np.float32(2.0 ** -6)] = 0
    return v.astype(BF)
def same(t):
    return np.repeat(t[None], N, axis=0)
def only(t, k):
    t = np.array(t)
    t[:, 4 * k:] = 0
    return t
def plain(rng):
    return {"x": f(rng, N, 128, 4 * T), "gr": big(f(rng, N, 128, 4 * T), 8), "rt": same(only(f(rng, 128, 512), N)), "w": f(rng, N, 128, 2048), "ub": big(f(rng, N, 128, 2048), 4), "pr": same(only(f(rng, 128, 512), 1)), "v": f(rng, N, 128, 512)}
def deal(rng, n, among):
    m, j, p = len(among), np.arange(n), rng.permutation(among)
    return np.stack([p[j % m], p[(j + 1 + j // m % (m - 1)) % m]], axis=1)
def routed(rng, to, far=False):
    g = np.arange(128) // (128 // N)
    rt = np.zeros((128, 128, 4), np.float32)
    rt[np.arange(128), g, 0] = 1 + rng.random(128)
    x = rng.standard_normal((N, 128, T, 4)) * (2 if far else 8)
    low = 0.125 * rng.choice([-1.0, 1.0], (N, 128, T))
    first, second = to[:, None, :, 0] == g[None, :, None], to[:, None, :, 1] == g[None, :, None]
    size = np.where(first, low, np.where(second, -4.0, -16.0)) if far else np.where(first, 16.0, np.where(second, 2.0, low))
    x[..., 0] = size * (1 + rng.random((N, 128, T)))
    if far: x, rt = x * 2.0 ** 25, rt * np.float32(2.0 ** 29)
    return {"x": mx_ref.flush(x.reshape(N, 128, 4 * T).astype(np.float32).astype(BF)), "rt": same(rt.reshape(128, 512).astype(BF))}
def setup_inputs(rng):
    return plain(rng)
def setup_inputs_crowd(rng):
    h = int(rng.integers(0, N))
    rest, n, to = np.delete(np.arange(N), h), [CAPP, T, CAPP + 1, CAPR, 0, CAPR + 1, CAPR - 1, 1], np.zeros((N, T, 2), int)
    for i in range(N):
        t = deal(rng, T, rest)
        t[np.arange(n[i]), rng.integers(0, 2, n[i])] = h
        to[(h + 1 + i) % N] = t[rng.permutation(T)]
    d = {**plain(rng), **routed(rng, to)}
    sign, pr = rng.choice([-1.0, 1.0], (128, 1, 4)), np.zeros((128, 128, 4), np.float32)
    pr[:, :1] = 2.0 ** 29 * sign * (1 + rng.random((128, 1, 4)))
    gr = 2.0 ** 28 * sign[None] * (1 + rng.random((N, 128, T, 4))) * rng.choice([-1.0, 1.0], (N, 1, T, 1))
    d["pr"] = same(pr.reshape(128, 512).astype(BF))
    d["gr"] = gr.reshape(N, 128, 4 * T).astype(np.float32).astype(BF)
    d["ub"] = (d["ub"].astype(np.float32) * np.float32(2.0 ** -22)).astype(BF)
    return d
def setup_inputs_dead(rng):
    rest = np.delete(np.arange(N), int(rng.integers(0, N)))
    to, dead = np.zeros((N, T, 2), int), np.zeros((N, T), bool)
    for q in range(N):
        s = rng.permutation(T)
        to[q] = deal(rng, T, rest)[s]
        dead[q] = s // (N - 1) % 4 != 0
    d = {**plain(rng), **routed(rng, to)}
    x = d["x"].astype(np.float32).reshape(N, 128, T, 4)
    x[..., 1:] = 16 * (1 + rng.random((N, 128, T, 3))) * np.where(dead, 1.0, -1.0)[:, None, :, None]
    d["x"] = x.reshape(N, 128, 4 * T).astype(BF)
    w = np.array(d["w"])
    w[rng.permutation(rest)[:N // 2]] = (-1 - rng.random((N // 2, 128, 2048))).astype(np.float32).astype(BF)
    d["w"] = w
    return d
def setup_inputs_one(rng):
    h = int(rng.integers(0, N))
    to = np.full((N, T, 2), h)
    for q in range(N): to[q, :, 1] = rng.permutation(deal(rng, T, np.delete(np.arange(N), h))[:, 0])
    return {**plain(rng), **routed(rng, to, far=True)}
def setup_inputs_spread(rng):
    d = plain(rng)
    x = (wide(rng, N, 128, 4 * T, cols=6).astype(np.float32) * np.float32(2.0 ** 8)).reshape(N, 128, T, 4)
    for q in range(N):
        i = rng.permutation(T)[:T // 8]
        x[q][:, i] = 2.0 ** -29 * (1 + rng.random((128, i.size, 4))) * rng.choice([-1.0, 1.0], (128, i.size, 4))
    d["x"] = x.reshape(N, 128, 4 * T).astype(BF)
    d["rt"] = (d["rt"].astype(np.float32) * np.float32(2.0 ** 20)).astype(BF)
    d["gr"] = big(wide(rng, N, 128, 4 * T, cols=3), 16)
    return d
def setup_inputs_ties(rng):
    u, o = sorted(rng.permutation(N)[:2].tolist())
    rest = np.delete(np.arange(N), [u, o])
    to, at = np.zeros((N, T, 2), int), []
    for q in range(N):
        t, s = deal(rng, T, rest), rng.permutation(T)
        t[:T // 2] = np.array([u, rest[0]])
        t[T // 2:T // 2 + 4, 1] = u
        to[q] = t[s]
        at.append(np.flatnonzero(s < T // 2))
    d = {**plain(rng), **routed(rng, to)}
    r = np.array(d["rt"]).reshape(N, 128, 128, 4)
    r[:, :, o] = r[:, :, u]
    x, g = d["x"].astype(np.float32).reshape(N, 128, T, 4), d["gr"].astype(np.float32).reshape(N, 128, T, 4)
    for q in range(N):
        i = at[q]
        x[q][:, i] = x[q][:, i[:1]].copy()
        g[q][:, i] = g[q][:, i[:1]].copy() * rng.choice([-1.0, 1.0], i.size)[None, :, None]
    return {**d, "x": x.reshape(N, 128, 4 * T).astype(BF), "gr": g.reshape(N, 128, 4 * T).astype(BF), "rt": r.reshape(N, 128, 512)}
def check_inputs(d):
    b = []
    for k in ("x", "gr", "rt", "w", "ub", "pr", "v"):
        a = np.abs(d[k].astype(np.float32))
        if not (np.isfinite(a).all() and ((a == 0) | (a >= 2.0 ** -30) & (a <= 2.0 ** 30)).all()): b.append("a value of " + k)
    for k, n in (("rt", N), ("pr", 1)):
        a = d[k].astype(np.float32)
        if (a != a[:1]).any(): b.append(k + " differs between ranks")
        if (a[:, :, 4 * n:] != 0).any(): b.append(k + " has numbers behind its first columns")
    return b
def reference(x, gr, rt, w, ub, pr, v):
    qz = lambda t: mx_ref.quantize(np.ascontiguousarray(t))
    to = []
    for q in range(N):
        s = mx_ref.matmul(qz(rt[q]), qz(x[q]))[:N] + np.float32(0)
        to.append(np.argsort(-s, axis=0, kind="stable")[:2])
    everyx, everyg = np.concatenate([x[q] for q in range(N)], axis=1), np.concatenate([gr[q] for q in range(N)], axis=1)
    came = np.zeros((N, 128, 2 * T, 4), np.float32)
    ct = np.zeros((N, 1, T), np.float32)
    for e in range(N):
        taken = [np.flatnonzero((to[q] == e).any(axis=0))[:CAPP] for q in range(N)]
        at = np.full((N, CAPP), -1)
        for q in range(N): at[q, :taken[q].size] = T * q + taken[q]
        at = at.reshape(-1)
        xs, gs = qz(cols(everyx, at)), qz(cols(everyg, at))
        forward = np.stack([mx_ref.matmul(qz(cut(w[e], i)), xs) for i in range(4)], axis=2).reshape(128, -1)
        m = qz(np.where(forward > 0, decode(gs), np.float32(0)).astype(BF))
        strength = np.abs(mx_ref.matmul(qz(pr[e]), m)[0])
        dx = decode(qz(tile([mx_ref.matmul(qz(cut(ub[e], i)), m) * np.float32(0.0625) for i in range(4)]))).reshape(128, -1, 4)
        for q in range(N):
            k = np.argsort(-strength[CAPP * q:CAPP * q + taken[q].size], kind="stable")[:CAPR]
            j = taken[q][k]
            second = (to[q][1, j] == e).astype(int)
            came[q][:, T * second + j] = dx[:, CAPP * q + k]
            ct[q, 0, j] += 1 + second
    oc, osc, y = np.zeros((N, 128, 4 * T), np.uint8), np.zeros((N, 16, T), np.uint8), np.zeros((N, 128, T), np.float32)
    for q in range(N):
        z = qz((came[q][:, :T] + came[q][:, T:]).reshape(128, 4 * T).astype(BF))
        oc[q], osc[q] = emit(z)
        y[q] = mx_ref.matmul(qz(v[q]), z)
    return {"oc": oc, "osc": osc, "ct": ct, "y": y}

@@ -1,0 +1,532 @@
+from concourse.bass import DstId, RemoteDMATransfer
+from concourse.mybir import dt, AluOpType, AxisListType, ActivationFunctionType
+
+A = AluOpType
+F = ActivationFunctionType
+BIG, FLOOR, TINY, MAGIC16, MAGIC1 = 1e29, -1e25, 2.0 ** -100, 1.5 * 2.0 ** 27, 1.5 * 2.0 ** 23
+
+SCRATCH = {}
+ALIAS = {}
+
+
+def _sb(name, n, d="float32"):
+    SCRATCH[name] = ("sbuf", [128, n], d)
+
+
+def _mx(name, n):
+    _sb(name, n, "float8_e4m3fn_x4")
+    _sb(name + "_s", n, "uint8")
+
+
+for _n, _w in (("xq", 664), ("tkq", 128), ("rq", 128), ("sl", 768), ("ld", 768), ("xg", 768), ("wq", 512),
+               ("uq", 512), ("prq", 128), ("ebq", 512), ("mq", 384), ("dxw", 516), ("blq", 144), ("ret", 192), ("rl", 152), ("rv", 160),
+               ("kq", 128), ("ahq", 160), ("ohq", 128), ("btq", 128), ("ctq", 128), ("zc", 256), ("zq", 128)):
+    _mx(_n, _w)
+for _n, _w in (("xt", 576), ("gt", 544), ("tri", 512), ("tk", 512), ("br", 704), ("wb", 2048), ("ubb", 2048), ("bv", 640),
+               ("pb", 4), ("bp", 640), ("eye", 520), ("mt", 1536), ("dxt", 1536), ("at", 528), ("aht", 640),
+               ("oht", 512), ("zt", 512), ("ti", 128), ("e128", 128), ("rp", 128), ("tmpc", 128), ("oa", 384),
+               ("oh", 384), ("mk", 1536), ("sg", 768), ("junk", 384), ("dd", 288), ("cmp", 288), ("cc", 288)):
+    _sb(_n, _w, "bfloat16")
+for _n, _w in (("sc", 32), ("pm", 40), ("cm", 16), ("ab", 8), ("iab", 4), ("acc", 4), ("n48", 48), ("ys", 96), ("t96", 96),
+               ("rk", 4), ("tok", 4), ("nt", 4), ("mp", 4), ("mm_", 4), ("m16", 4), ("m18", 4), ("rr_", 4), ("wk", 4), ("w18", 4),
+               ("cd", 4), ("rkh", 4), ("ysb", 128), ("ctsb", 128)):
+    _sb(_n, _w)
+_at = 0
+for _n, _w in (("em16", 16), ("emv", 16), ("g48", 48), ("bi", 16), ("bib", 16), ("d16", 16), ("cp16", 16), ("s96", 96), ("h96", 96),
+               ("o96", 96), ("fx", 48)):
+    ALIAS[_n] = ("cs", _at)
+    _at += _w
+_sb("cs", _at)
+for _n, _b, _o in (("bt", "br", 0), ("rst", "br", 192), ("blt", "bp", 0), ("prt", "bp", 128), ("bt2", "bv", 0)):
+    ALIAS[_n] = (_b, _o)
+_sb("pi", 8, "int32")
+for _n, _w in (("off", 48), ("ofs", 48), ("of2", 16), ("of3", 16)):
+    _sb(_n, _w, "uint16")
+for _k in range(8):
+    SCRATCH["ps%d" % _k] = ("psum", [128, 512], "float32")
+SEMAPHORES = ["sv", "ss", "st", "sg", "lx", "lrt", "lgr", "lpr", "lw", "lub", "lv", "arc", "arp", "owc", "owp", "rec", "rep", "orc", "orp",
+              "rkc", "rkp", "okc", "okp", "zrc", "zrp", "loc", "o_oc", "o_y", "o_ct", "o_s0", "o_s1", "o_s2", "o_s3"]
+
+
+def rank_program(g, core, T, topo):
+    q = T.rank_of(core)
+    if q is None:
+        return
+    N = len(T.cores)
+    eng = {"v": g.vector, "s": g.scalar, "t": g.tensor, "g": g, "y": g.sync}
+    own = {"v": "sv", "s": "ss", "t": "st", "g": "sg"}
+    total, snaps, log = {}, {}, {}
+    seen = {k: {} for k in eng}
+
+    def clash(a, b):
+        if a[2] <= b[1] or b[2] <= a[1]:
+            return False
+        return not (a[3] == b[3] > 1 and (a[1] - b[1]) % a[3])
+
+    def wait(qn, s, v):
+        if seen[qn].get(s, 0) >= v:
+            return
+        eng[qn].wait_ge(T.sem[s], v)
+        seen[qn][s] = v
+        for k, w in snaps.get((s, v), {}).items():
+            seen[qn][k] = max(seen[qn].get(k, 0), w)
+
+    def depend(qn, reads, writes, dma=False):
+        need = {}
+        for acc, w in [(r, False) for r in reads] + [(r, True) for r in writes]:
+            bank = acc[0][:2] == "ps" and len(acc[0]) == 3
+            for rec in log.get(acc[0], []):
+                if not bank and not clash(acc, rec[0]):
+                    continue
+                if not (w or rec[1] or (bank and rec[2] != qn)):
+                    continue
+                if rec[2] == qn and not dma and (not rec[1] or (qn == "t" and bank)):
+                    continue
+                need[rec[3]] = max(need.get(rec[3], 0), rec[4])
+        for s, v in need.items():
+            wait(qn, s, v)
+
+    def note(who, reads, writes, s, v):
+        for r in writes:
+            if r[3] == 1:
+                log[r[0]] = [k for k in log.get(r[0], []) if not (r[1] <= k[0][1] and k[0][2] <= r[2])]
+        for acc, w in [(r, False) for r in reads] + [(r, True) for r in writes]:
+            log.setdefault(acc[0], []).append((acc, w, who, s, v))
+
+    def op(qn, reads, writes, call):
+        depend(qn, reads, writes)
+        s = own[qn]
+        call().then_inc(T.sem[s], 1)
+        total[s] = total.get(s, 0) + 1
+        snaps[(s, total[s])] = dict(seen[qn])
+        note(qn, reads, writes, s, total[s])
+
+    def dma(qn, reads, writes, out, in_, s):
+        depend(qn, reads, writes, dma=True)
+        eng[qn].dma_start(out, in_).then_inc(T.sem[s], 16)
+        total[s] = total.get(s, 0) + 16
+        snaps[(s, total[s])] = dict(seen[qn])
+        note("dma", reads, writes, s, total[s])
+
+    def R(name, lo, hi, step=1):
+        b, o = ALIAS.get(name, (name, 0))
+        return (b, lo + o, hi + o, step)
+
+    def ap(r):
+        return T[r[0]][:, r[1]:r[2]] if r[3] == 1 else T[r[0]][:, r[1]:r[2]:r[3]]
+
+    def sc_(v):
+        return ap(v) if isinstance(v, tuple) else v
+
+    def rds(*vs):
+        return [v for v in vs if isinstance(v, tuple)]
+
+    def ts(out, in0, s1, s2, op0, op1=None):
+        if op1 is None:
+            op("v", rds(in0, s1), [out], lambda: g.vector.tensor_scalar(ap(out), ap(in0), sc_(s1), None, op0))
+        else:
+            op("v", rds(in0, s1, s2), [out], lambda: g.vector.tensor_scalar(ap(out), ap(in0), sc_(s1), sc_(s2), op0, op1))
+
+    def tt(out, a, b, o):
+        op("v", [a, b], [out], lambda: g.vector.tensor_tensor(ap(out), ap(a), ap(b), o))
+
+    def cp(out, a):
+        op("v", [a], [out], lambda: g.vector.tensor_copy(ap(out), ap(a)))
+
+    def ms(out, c):
+        op("v", [], [out], lambda: g.vector.memset(ap(out), c))
+
+    def red(out, a, o):
+        op("v", [a], [out], lambda: g.vector.tensor_reduce(ap(out), ap(a), AxisListType.X, o))
+
+    def scan(out, a, z, o0, o1):
+        op("v", [a, z], [out], lambda: g.vector.tensor_tensor_scan(ap(out), ap(a), ap(z), -9e29, o0, o1))
+
+    def qz(name, lo, n, tile, t0=0):
+        r = R(tile, t0, t0 + 4 * n)
+        op("v", [r], [R(name, lo, lo + n), R(name + "_s", lo, lo + n)],
+           lambda: g.vector.quantize_mx(T[name][:, lo:lo + n], T[name + "_s"][:, lo:lo + n], ap(r)))
+
+    def act(out, a, f, scale=1.0, bias=0.0, acc=None):
+        if acc is None:
+            op("s", rds(a, scale, bias), [out], lambda: g.scalar.activation(ap(out), ap(a), f, bias=sc_(bias), scale=sc_(scale)))
+        else:
+            op("s", rds(a, scale, bias), [out, acc],
+               lambda: g.scalar.activation(ap(out), ap(a), f, bias=sc_(bias), scale=sc_(scale), accum_out=ap(acc)))
+
+    def zero(name, lane, hi=512, lo=0):
+        act(R(name, lo + lane, hi, 4), R("ti", 0, 128), F.Copy, 0.0)
+
+    def mm(bank, lhs, l0, rhs, r0, n, start=True, stop=True):
+        op("t", [R(lhs, l0, l0 + 128), R(lhs + "_s", l0, l0 + 128), R(rhs, r0, r0 + n), R(rhs + "_s", r0, r0 + n)], [R(bank, 0, n)],
+           lambda: g.tensor.matmul_mx(T[bank][:, 0:n], T[lhs][:, l0:l0 + 128], T[lhs + "_s"][:, l0:l0 + 128],
+                                      T[rhs][:, r0:r0 + n], T[rhs + "_s"][:, r0:r0 + n], start, stop))
+
+    def pickc(out, o0, n, win, w0, w1, off, f0):
+        fr = R(off, f0, f0 + n // 16)
+        op("v", [R(win, w0, w1), fr], [R(out, o0, o0 + n)],
+           lambda: g.vector.tensor_copy(T[out][:, o0:o0 + n].bitcast(dt.uint32), T[win][:, w0:w1].bitcast(dt.uint32).indirect(ap(fr))))
+
+    def picks(out, o0, n, win, w0, w1, off, f0):
+        fr = R(off, f0, f0 + n // 16)
+        op("s", [R(win + "_s", w0, w1), fr], [R(out + "_s", o0, o0 + n)],
+           lambda: g.scalar.activation(T[out + "_s"][:, o0:o0 + n], T[win + "_s"][:, w0:w1].indirect(ap(fr)), F.Copy))
+
+    def pick(*a):
+        pickc(*a)
+        picks(*a)
+
+    def iota(name, n, pattern, cm=0):
+        r = R(name, 0, n)
+        op("g", [], [r], lambda: g.iota(ap(r), pattern, 0, cm, allow_small_or_imprecise_dtypes=True))
+
+    peers = [c for c in T.cores if c != core]
+    far = [c for c in peers if topo.die(c) != topo.die(core)]
+    near = [c for c in peers if c not in far]
+    masks = {}
+    for group, first in ((far, 0), (near, 1)):
+        for j, c in enumerate(group):
+            e = topo.engines(core, c)[first::2]
+            masks[c] = (1 << e[2 * j]) | (1 << e[2 * j + 1])
+
+    def send(src, start, width, dst, s, code, to):
+        blocks = [R(src, start(T.rank_of(c)), start(T.rank_of(c)) + width) for c in to]
+        depend("g", blocks, [])
+        ts_ = []
+        for c, r in zip(to, blocks):
+            rid, pid = topo.addr(c)[:2]
+            a, b = ap(r), T[dst][:, width * q:width * q + width]
+            if code:
+                a, b = a.bitcast(dt.uint8), b.bitcast(dt.uint8)
+            ts_.append(RemoteDMATransfer(dst_ids=[DstId(rid=rid, pnc=pid)], dma_engine_mask=masks[c], remote_sem=T.sem[s], src=a, dst=b))
+        g.remote_dma_fused(ts_, local_sem=T.sem["loc"])
+        total["loc"] = total.get("loc", 0) + 2 * len(to)
+        note("dma", blocks, [], "loc", total["loc"])
+
+    def arrives(dst, dw, s):
+        total[s] = 2 * len(peers)
+        for e in range(N):
+            if e != q:
+                note("dma", [], [R(dst, dw * e, dw * (e + 1))], s, total[s])
+
+    def localcopy(src, a, dst, b, width, s, code):
+        i, o = T[src][:, a:a + width], T[dst][:, b:b + width]
+        if code:
+            i, o = i.bitcast(dt.uint8), o.bitcast(dt.uint8)
+        dma("y", [R(src, a, a + width)], [R(dst, b, b + width)], o, i, s)
+
+    def load(qn, name, w, src, s, at=0):
+        r = R(name, at, at + w)
+        dma(qn, [], [r], ap(r), src, s)
+
+    load("y", "xt", 512, T.x[:, :], "lx")
+    load("s", "xt", 32, T.rt[:, 0:32], "lrt", 544)
+    load("y", "gt", 512, T.gr[:, :], "lgr")
+    load("s", "pb", 4, T.pr[:, 0:4], "lpr")
+    load("y", "wb", 2048, T.w[:, :], "lw")
+    load("s", "ubb", 2048, T.ub[:, :], "lub")
+    load("y", "bv", 512, T.v[:, :], "lv", 128)
+
+    iota("pi", 1, [[1, 1]], cm=1)
+    iota("ti", 128, [[1, 128]])
+    iota("rp", 128, [[0, 8], [1, 16]])
+    iota("bi", 3, [[16, 3]])
+    iota("em16", 16, [[1, 8], [0, 2]])
+    iota("g48", 48, [[1, 8], [100, 2], [0, 3]])
+    iota("e128", 128, [[1, 8], [0, 16]])
+    iota("fx", 48, [[16, 3], [48, 2], [96, 8]])
+    iota("d16", 12, [[32, 4], [8, 3]])
+    iota("s96", 96, [[16, 3], [0, 2], [1, 16]])
+    iota("h96", 96, [[0, 3], [1, 2], [0, 16]])
+    iota("cp16", 16, [[18, 2], [1, 8]])
+    iota("blt", 128, [[0, 128]])
+    col = lambda k: R("sc", k, k + 1)
+    pF, iF, eF, hF, e100, iH, flag, e16, eh, el, qsel = [col(k) for k in (0, 1, 2, 3, 5, 6, 7, 8, 12, 13, 14)]
+    TI, RP, E128 = R("ti", 0, 128), R("rp", 0, 128), R("e128", 0, 128)
+    p0 = R("pi", 0, 1)
+    ms(R("xt", 512, 544), 0.0)
+    ms(R("pm", 0, 40), FLOOR)
+    ms(R("gt", 512, 544), 0.0)
+    ts(R("pi", 1, 2), p0, 15, None, A.bitwise_and)
+    ts(R("pi", 2, 3), p0, 4, None, A.arith_shift_right)
+    ts(R("pi", 3, 4), p0, 4, 1, A.arith_shift_right, A.bitwise_and)
+    ms(R("eye", 0, 520), 0.0)
+    cp(R("sc", 0, 4), R("pi", 0, 4))
+    ts(R("eye", 4, 516, 4), TI, pF, None, A.is_equal)
+    for lane in range(4):
+        ts(R("tri", lane, 512, 4), TI, pF, None, A.is_ge)
+    for lane in range(4):
+        ts(R("rst", lane, 512, 4), RP, iF, None, A.is_equal)
+    zero("tk", 2)
+    zero("tk", 3)
+    zero("oht", 3)
+    zero("aht", 3, 640, 128)
+    act(R("aht", 0, 128), TI, F.Copy, 0.0)
+    act(e100, eF, F.Identity, 1.0, 100.0)
+    act(iH, iF, F.Identity, 1.0, 0.5)
+    act(e16, eF, F.Copy, 16.0)
+    act(R("bib", 0, 3), R("bi", 0, 3), F.Identity, 1.0, iH)
+    qz("xq", 128, 144, "xt")
+    mm("ps0", "xq", 128, "xq", 144, 128)
+    qz("xq", 272, 128, "tri")
+    qz("ebq", 0, 128, "eye", 4)
+    ts(R("bt", 2, 192, 4), R("g48", 0, 48), e100, 512.0, A.is_equal, A.mult)
+    act(R("bt", 3, 192, 4), R("bt", 2, 192, 4), F.Copy, 0.0625)
+
+    S = R("ps0", 120, 128)
+    ts(R("emv", 0, 16), R("em16", 0, 16), eF, None, A.is_equal)
+    scan(R("pm", 1, 9), S, R("pm", 32, 40), A.max, A.max)
+    act(R("junk", 0, 8), R("pm", 1, 9), F.Sign, -1.0, R("pm", 8, 9), R("iab", 0, 1))
+    ts(R("cm", 0, 8), R("pm", 1, 9), R("pm", 8, 9), BIG, A.is_lt, A.mult)
+    tt(R("ab", 0, 8), R("cm", 0, 8), R("pm", 0, 8), A.add)
+    scan(R("pm", 17, 25), S, R("ab", 0, 8), A.max, A.min)
+    act(R("junk", 8, 16), R("pm", 17, 25), F.Sign, -1.0, R("pm", 24, 25), R("iab", 1, 2))
+    ts(R("tk", 0, 512, 4), E128, R("iab", 0, 1), None, A.is_equal)
+    ts(R("tk", 1, 512, 4), E128, R("iab", 1, 2), None, A.is_equal)
+    qz("tkq", 0, 128, "tk")
+
+    k3 = lambda n: R(n, 0, 3)
+    mm("ps1", "tkq", 0, "xq", 270, 130)
+    mm("ps2", "tkq", 0, "xq", 270, 130)
+    qz("rq", 0, 128, "rst")
+    qz("xq", 400, 136, "gt")
+    qz("ebq", 128, 128, "eye", 3)
+    for k in range(2):
+        act(R("junk", 16 + 128 * k, 144 + 128 * k), R("ps1", 2, 130), F.Sign, -1.0, R("bib", k, k + 1), R("acc", k, k + 1))
+    ts(R("tmpc", 0, 128), R("ps2", 2, 130), R("bib", 2, 3), 0.5, A.is_lt, A.subtract)
+    ts(R("ofs", 0, 48), R("fx", 0, 48), iF, None, A.add)
+    red(R("acc", 2, 3), R("tmpc", 0, 128), A.add)
+    for k in range(2):
+        act(R("n48", k, 48, 3), R("emv", 0, 16), F.Copy, R("acc", k, k + 1))
+    ts(R("prt", 0, 512, 4), TI, 0.0, R("pb", 0, 1), A.mult, A.add)
+    ts(R("n48", 2, 48, 3), R("emv", 0, 16), R("acc", 2, 3), 2.0, A.mult, A.mult)
+    ts(R("prt", 1, 512, 4), TI, 0.0, R("pb", 1, 2), A.mult, A.add)
+    ts(R("bt", 0, 192, 4), R("n48", 0, 48), MAGIC16, MAGIC16, A.add, A.subtract)
+    ts(R("prt", 2, 512, 4), TI, 0.0, R("pb", 2, 3), A.mult, A.add)
+    tt(R("bt", 1, 192, 4), R("n48", 0, 48), R("bt", 0, 192, 4), A.subtract)
+    ts(R("prt", 3, 512, 4), TI, 0.0, R("pb", 3, 4), A.mult, A.add)
+    qz("xq", 536, 128, "bt")
+    mm("ps4", "rq", 0, "xq", 526, 128)
+    for b in (2, 3):
+        qz("ebq", 128 * b, 128, "eye", 4 - b)
+    ts(R("off", 0, 48), R("ps4", 10, 58), 0.5, 64.0, A.mult, A.add)
+    act(R("s96", 0, 96), R("s96", 0, 96), F.Copy, -TINY)
+    act(R("sc", 9, 12), R("bib", 0, 3), F.Identity, TINY, -0.5 * TINY)
+    act(R("tok", 0, 2), R("acc", 0, 2), F.Identity, 0.5, 64.0)
+    act(R("tok", 2, 3), R("acc", 2, 3), F.Identity, 1.0, 64.0)
+    act(k3("nt"), k3("tok"), F.Copy, -1.0)
+    act(k3("mp"), k3("tok"), F.Identity, 0.0625, -0.46875)
+    for k in range(3):
+        act(R("oa", 128 * k, 128 * k + 128), TI, F.Abs, 1.0, R("nt", k, k + 1))
+
+    there = [T.rank_of(c) for c in far]
+    for group in (there[:2], there[2:], [e for e in range(N) if e not in there]):
+        for e in group:
+            if e - 1 not in group:
+                n = 1
+                while e + n in group:
+                    n += 1
+                pick("sl", 96 * e, 96 * n, "xq", 128, 536, "off", 6 * e)
+    out = lambda e: 96 * e
+    for to in (far[:2], far[2:], near):
+        send("sl", out, 96, "ld", "arc", True, to)
+    send("sl_s", out, 96, "ld_s", "arp", False, peers)
+    localcopy("sl", 96 * q, "ld", 96 * q, 96, "owc", True)
+    localcopy("sl_s", 96 * q, "ld_s", 96 * q, 96, "owp", False)
+    localcopy("xq", 256, "rl", 144, 8, "zrc", True)
+    localcopy("xq_s", 256, "rl_s", 144, 8, "zrp", False)
+    arrives("ld", 96, "arc")
+    arrives("ld_s", 96, "arp")
+
+    iota("bt2", 128, [[0, 128]])
+    qz("prq", 0, 128, "prt")
+    ts(R("tri", 0, 512, 4), TI, pF, None, A.is_equal)
+    ts(R("tri", 1, 512, 4), TI, pF, 2.0, A.is_equal, A.mult)
+    ts(R("o96", 0, 96), R("h96", 0, 96), hF, -BIG, A.not_equal, A.mult)
+    ts(R("at", 3, 512, 4), RP, pF, None, A.is_equal)
+    qz("xq", 0, 128, "tri")
+    ms(R("at", 512, 528), 0.0)
+    ts(flag, pF, float(q), 64.0, A.not_equal, A.mult)
+    tt(R("o96", 0, 96), R("o96", 0, 96), R("s96", 0, 96), A.add)
+    D16 = R("d16", 0, 12)
+    ts(R("blt", 1, 48, 4), D16, e16, 128.0, A.is_equal, A.mult)
+    ts(R("blt", 64, 112, 4), D16, e16, iF, A.is_equal, A.mult)
+    mm("ps3", "tkq", 0, "xq", 0, 130)
+    for k in range(3):
+        act(R("oh", 128 * k, 128 * k + 128), R("oa", 128 * k, 128 * k + 128), F.Relu, -1.0, 1.0)
+    act(R("blt", 2, 48, 4), R("blt", 1, 48, 4), F.Copy, 2.0)
+    act(R("blt", 3, 48, 4), D16, F.Copy)
+    for k in (1, 2):
+        act(R("blt", 64 + k, 112, 4), R("blt", 64, 112, 4), F.Copy)
+    act(R("at", 517, 528, 4), R("ti", 0, 3), F.Identity, 0.0, flag)
+    for k in range(3):
+        act(R("cc", 96 * k, 96 * k + 96), R("o96", 0, 96), F.Identity, 1.0, col(9 + k))
+    qz("wq", 0, 512, "wb")
+    ms(R("blt", 7, 48, 12), 512.0)
+    ts(k3("mm_"), k3("mp"), MAGIC1, MAGIC1, A.add, A.subtract)
+    for k in range(3):
+        tt(R("oht", k, 512, 4), R("ps3", 0, 128), R("oh", 128 * k, 128 * k + 128), A.mult)
+    qz("uq", 0, 512, "ubb")
+    qz("blq", 0, 144, "blt")
+    act(k3("m16"), k3("mm_"), F.Copy, -16.0)
+    act(k3("m18"), k3("mm_"), F.Identity, 1.0, -18.0)
+    ts(qsel, eF, float(q), None, A.is_equal)
+    ts(eh, eF, 8.0, 16.0, A.subtract, A.mult)
+    ts(el, eF, 8.0, 2.0, A.subtract, A.mult)
+    ts(R("tk", 1, 512, 4), E128, pF, None, A.is_equal)
+    ts(R("tk", 0, 512, 4), RP, iF, qsel, A.is_equal, A.mult)
+    tt(k3("rr_"), k3("m16"), k3("tok"), A.add)
+    qz("rv", 32, 128, "bv", 128)
+    qz("kq", 0, 128, "tk")
+
+    MK = lambda b, o: R("mk", 384 * b + o, 384 * b + o + 128)
+    pick("xg", 0, 128, "ld", 0, 768, "ofs", 0)
+    pick("xg", 128, 128, "ld", 0, 768, "ofs", 8)
+    pick("xg", 256, 256, "ld", 0, 768, "ofs", 16)
+    pickc("xg", 512, 256, "ld", 0, 768, "ofs", 32)
+    for o in (0, 128, 256):
+        for i in range(4):
+            mm("ps%d" % i, "wq", 128 * i, "xg", 2 * o, 128)
+        for b in range(4):
+            mm("ps%d" % (4 + b), "ebq", 128 * b, "xg", 2 * o + 128, 128)
+        for b in (0, 2):
+            ts(MK(b, o), R("ps%d" % b, 0, 128), 0.0, None, A.is_gt)
+        for j, b in enumerate((1, 3)):
+            act(R("sg", 384 * j + o, 384 * j + o + 128), R("ps%d" % b, 0, 128), F.Sign)
+            act(MK(b, o), R("sg", 384 * j + o, 384 * j + o + 128), F.Relu)
+        if o == 0:
+            picks("xg", 512, 256, "ld", 0, 768, "ofs", 32)
+        for b in range(4):
+            tt(R("mt", 4 * o + b, 4 * o + 512, 4), R("ps%d" % (4 + b), 0, 128), MK(b, o), A.mult)
+        qz("mq", o, 128, "mt", 4 * o)
+
+    parts = ((0, 256), (256, 128))
+    UB = (("ps2", "ps3", "ps5", "ps6"), ("ps7", "ps0", "ps1", "ps4"))
+
+    def product(h, i):
+        mm(UB[h][i], "uq", 128 * i, "mq", parts[h][0], parts[h][1])
+
+    def shrink(qn, h, i):
+        o, n = parts[h]
+        if qn == "s":
+            act(R("dxt", 4 * o + i, 4 * (o + n), 4), R(UB[h][i], 0, n), F.Copy, 0.0625)
+        else:
+            ts(R("dxt", 4 * o + i, 4 * (o + n), 4), R(UB[h][i], 0, n), 0.0625, None, A.mult)
+
+    D = lambda k, a, b: R("dd", 96 * k + a, 96 * k + b)
+    C = lambda k, a, b: R("cmp", 96 * k + a, 96 * k + b)
+    CC = lambda k, a, b: R("cc", 96 * k + a, 96 * k + b)
+    st = lambda k: R("ys", 32 * k, 32 * k + 1)
+    rk = lambda k: R("rk", k, k + 1)
+
+    def turn(a, b):
+        op("v", [R("ys", a, b)], [R("t96", a, b)], lambda: g.vector.transpose(T.t96[:, a:b], T.ys[:, a:b]))
+
+    def less(k, a, b):
+        act(D(k, a, b), R("t96", a, b), F.Identity, -1.0, st(k))
+
+    for k in (0, 1):
+        mm("ps%d" % k, "mq", 128 * k, "prq", 0, 128)
+    product(0, 0)
+    for k in (0, 1):
+        act(R("ys", 32 * k, 32 * k + 32), R("ps%d" % k, 0, 32), F.Abs)
+    mm("ps4", "mq", 256, "prq", 0, 128)
+    for i in (1, 2, 3):
+        product(0, i)
+    turn(0, 64)
+    shrink("v", 0, 0)
+    for k in (0, 1):
+        less(k, 0, 64)
+    tt(C(0, 0, 64), D(0, 0, 64), CC(0, 0, 64), A.is_lt)
+    act(R("ys", 64, 96), R("ps4", 0, 32), F.Abs)
+    for i in range(4):
+        product(1, i)
+    turn(64, 96)
+    for k in (0, 1):
+        less(k, 64, 96)
+    ts(D(2, 0, 96), R("t96", 0, 96), st(2), -1.0, A.subtract, A.mult)
+    tt(C(1, 0, 64), D(1, 0, 64), CC(1, 0, 64), A.is_lt)
+    for k in (0, 1):
+        tt(C(k, 64, 96), D(k, 64, 96), CC(k, 64, 96), A.is_lt)
+    tt(C(2, 0, 96), D(2, 0, 96), CC(2, 0, 96), A.is_lt)
+    shrink("s", 0, 1)
+    for k in (0, 1):
+        act(R("junk", 96 * k, 96 * k + 96), C(k, 0, 96), F.Copy, acc=rk(k))
+    red(rk(2), C(2, 0, 96), A.add)
+    for k in (0, 1, 2):
+        ts(R("at", k, 512, 4), RP, rk(k), None, A.is_equal)
+    ts(R("at", 516, 528, 4), R("rk", 0, 3), 16.0, None, A.min)
+    qz("dxw", 384, 132, "at")
+    ahead = lambda d: 512
+    send("dxw", ahead, 4, "rv", "rkc", True, peers)
+    send("dxw_s", ahead, 4, "rv_s", "rkp", False, peers)
+    localcopy("dxw", 512, "rv", 4 * q, 4, "okc", True)
+    localcopy("dxw_s", 512, "rv_s", 4 * q, 4, "okp", False)
+    arrives("rv", 4, "rkc")
+    arrives("rv_s", 4, "rkp")
+    mm("ps2", "dxw", 384, "blq", 0, 128, True, False)
+    mm("ps2", "dxw", 384, "blq", 16, 128, False, True)
+    shrink("s", 0, 2)
+    shrink("s", 0, 3)
+    qz("dxw", 0, 256, "dxt")
+    for i in range(3):
+        shrink("s", 1, i)
+    shrink("v", 1, 3)
+    qz("dxw", 256, 128, "dxt", 1024)
+    cp(R("of2", 0, 12), R("ps2", 0, 12))
+    pick("ret", 0, 192, "dxw", 0, 516, "of2", 0)
+
+    back = lambda d: 24 * d if d % 2 == 0 else 24 * d + 6
+    send("ret", back, 18, "rl", "rec", True, peers)
+    send("ret_s", back, 18, "rl_s", "rep", False, peers)
+    localcopy("ret", back(q), "rl", 18 * q, 18, "orc", True)
+    localcopy("ret_s", back(q), "rl_s", 18 * q, 18, "orp", False)
+    arrives("rl", 18, "rec")
+    arrives("rl_s", 18, "rep")
+    first = 0 if q % 2 == 0 else 2
+
+    for k in range(3):
+        act(R("junk", 128 * k, 128 * k + 128), R("oht", k, 512, 4), F.Copy, acc=R("wk", k, k + 1))
+    act(k3("w18"), k3("wk"), F.Copy, 18.0)
+    for k in range(3):
+        ts(R("aht", 128 + k, 640, 4), RP, R("rr_", k, k + 1), None, A.is_equal)
+    tt(k3("cd"), k3("w18"), k3("m18"), A.add)
+    for k in range(3):
+        ts(R("aht", k, 64, 4), R("cp16", 0, 16), R("cd", k, k + 1), eh, A.is_equal, A.mult)
+        ts(R("aht", 64 + k, 128, 4), R("cp16", 0, 16), R("cd", k, k + 1), el, A.is_equal, A.mult)
+    qz("ahq", 0, 160, "aht")
+    mm("ps0", "kq", 0, "rv", 0, 128)
+    mm("ps1", "ahq", 32, "ahq", 0, 128, True, False)
+    mm("ps1", "ahq", 32, "ahq", 16, 128, False, False)
+    for k in range(3):
+        red(R("rkh", k, k + 1), R("ps0", 1 + k, 32, 4), A.min)
+    for k in range(3):
+        ts(R("bt2", k, 64, 4), R("cp16", 0, 16), R("cd", k, k + 1), R("rkh", k, k + 1), A.is_equal, A.mult)
+    qz("btq", 0, 128, "bt2")
+    mm("ps1", "ahq", 32, "btq", 0, 128, False, True)
+    qz("ohq", 0, 128, "oht")
+    ts(R("of3", 0, 16), R("ps1", 0, 16), 144.0 + first, None, A.add)
+
+    for h in range(2):
+        pick("zc", 128 * h, 128, "rl", 0, 152, "of3", 8 * h)
+        for b in range(4):
+            mm("ps%d" % (4 + b), "ebq", 128 * b, "zc", 128 * h, 128, h == 0, h == 1)
+    ts(R("bt2", 64, 67), k3("rkh"), 15.5, None, A.is_lt)
+    qz("ctq", 0, 128, "bt2")
+    mm("ps2", "ctq", 0, "ohq", 0, 128)
+    for b in (0, 2):
+        act(R("zt", b, 512, 4), R("ps%d" % (4 + b), 0, 128), F.Copy)
+    for b in (1, 3):
+        cp(R("zt", b, 512, 4), R("ps%d" % (4 + b), 0, 128))
+    qz("zq", 0, 128, "zt")
+    mm("ps3", "rv", 32, "zq", 0, 128)
+    act(R("ctsb", 0, 128), R("ps2", 0, 128), F.Copy)
+    dma("y", [R("zq", 0, 128)], [], T.oc[:, :], T.zq[:, 0:128].bitcast(dt.uint8), "o_oc")
+    for k in range(4):
+        dma("y" if k < 1 else "s", [R("zq_s", 0, 128)], [], T.osc[4 * k:4 * k + 4, 0:128], T.zq_s[32 * k:32 * k + 4, 0:128], "o_s%d" % k)
+    dma("s", [R("ctsb", 0, 128)], [], T.ct[:, :], T.ctsb[16:17, 0:128], "o_ct")
+    cp(R("ysb", 0, 128), R("ps3", 0, 128))
+    dma("y", [R("ysb", 0, 128)], [], T.y[:, :], T.ysb[:, 0:128], "o_y")
+
+    for s, v in total.items():
+        wait("g", s, v)

@@ -25,7 +25,7 @@ for _n, _w in (("xq", 664), ("tkq", 128), ("rq", 128), ("sl", 768), ("ld", 768),
 for _n, _w in (("xt", 576), ("gt", 544), ("tri", 512), ("tk", 512), ("br", 704), ("wb", 2048), ("ubb", 2048), ("bv", 640),
                ("pb", 4), ("bp", 640), ("eye", 520), ("mt", 1536), ("dxt", 1536), ("at", 528), ("aht", 640),
                ("oht", 512), ("zt", 512), ("ti", 128), ("e128", 128), ("rp", 128), ("tmpc", 128), ("oa", 384),
-               ("oh", 384), ("mk", 1536), ("sg", 768), ("junk", 384), ("dd", 288), ("cmp", 288), ("cc", 288)):
+               ("oh", 384), ("mk", 1536), ("sg", 1152), ("junk", 384), ("dd", 288), ("cmp", 288), ("cc", 288)):
     _sb(_n, _w, "bfloat16")
 for _n, _w in (("sc", 32), ("pm", 40), ("cm", 16), ("ab", 8), ("iab", 4), ("acc", 4), ("n48", 48), ("ys", 96), ("t96", 96),
                ("rk", 4), ("tok", 4), ("nt", 4), ("mp", 4), ("mm_", 4), ("m16", 4), ("m18", 4), ("rr_", 4), ("wk", 4), ("w18", 4),
@@ -44,7 +44,7 @@ for _n, _w in (("off", 48), ("ofs", 48), ("of2", 16), ("of3", 16)):
     _sb(_n, _w, "uint16")
 for _k in range(8):
     SCRATCH["ps%d" % _k] = ("psum", [128, 512], "float32")
-SEMAPHORES = ["sv", "ss", "st", "sg", "lx", "lrt", "lgr", "lpr", "lw", "lub", "lv", "arc", "arp", "owc", "owp", "rec", "rep", "orc", "orp",
+SEMAPHORES = ["sv", "ss", "st", "sg", "lx", "lrt", "lgr", "lpr", "lw", "lub", "lv", "arc", "arp", "rec", "rep", "orc", "orp",
               "rkc", "rkp", "okc", "okp", "zrc", "zrp", "loc", "o_oc", "o_y", "o_ct", "o_s0", "o_s1", "o_s2", "o_s3"]
 
 
@@ -182,29 +182,48 @@ def rank_program(g, core, T, topo):
 
     peers = [c for c in T.cores if c != core]
     far = [c for c in peers if topo.die(c) != topo.die(core)]
-    near = [c for c in peers if c not in far]
+    mine = [c for c in T.cores if c not in far]
+    near = [mine[(mine.index(core) + j) % len(mine)] for j in range(1, len(mine))]
+    bits = lambda es: sum(1 << e for e in es)
     masks = {}
     for group, first in ((far, 0), (near, 1)):
         for j, c in enumerate(group):
-            e = topo.engines(core, c)[first::2]
-            masks[c] = (1 << e[2 * j]) | (1 << e[2 * j + 1])
+            masks[c] = bits(topo.engines(core, c)[first::2][2 * j:2 * j + 2])
+    between = topo.engines(core, near[0])[1::2]
+    wide, thin = dict(masks), dict(masks)
+    wide[near[2]] = bits(between[4:8])
+    thin[near[0]], thin[near[1]], thin[near[2]] = bits(between[0:4]), bits(between[4:6]), bits(between[6:8])
+    count = lambda m: bin(m).count("1")
+    ident = lambda c: DstId(rid=topo.addr(c)[0], pnc=topo.addr(c)[1])
 
-    def send(src, start, width, dst, s, code, to):
+    def send(src, start, width, dst, s, code, to, use):
         blocks = [R(src, start(T.rank_of(c)), start(T.rank_of(c)) + width) for c in to]
         depend("g", blocks, [])
         ts_ = []
         for c, r in zip(to, blocks):
-            rid, pid = topo.addr(c)[:2]
             a, b = ap(r), T[dst][:, width * q:width * q + width]
             if code:
                 a, b = a.bitcast(dt.uint8), b.bitcast(dt.uint8)
-            ts_.append(RemoteDMATransfer(dst_ids=[DstId(rid=rid, pnc=pid)], dma_engine_mask=masks[c], remote_sem=T.sem[s], src=a, dst=b))
+            ts_.append(RemoteDMATransfer(dst_ids=[ident(c)], dma_engine_mask=use[c], remote_sem=T.sem[s], src=a, dst=b))
         g.remote_dma_fused(ts_, local_sem=T.sem["loc"])
-        total["loc"] = total.get("loc", 0) + 2 * len(to)
+        total["loc"] = total.get("loc", 0) + sum(count(use[c]) for c in to)
         note("dma", blocks, [], "loc", total["loc"])
 
-    def arrives(dst, dw, s):
-        total[s] = 2 * len(peers)
+    every = topo.mask(core, peers[0])
+
+    def spread(src, start, width, dst, s, code):
+        r = R(src, start, start + width)
+        depend("g", [r], [])
+        a, b = ap(r), T[dst][:, width * q:width * q + width]
+        if code:
+            a, b = a.bitcast(dt.uint8), b.bitcast(dt.uint8)
+        g.remote_dma_fused([RemoteDMATransfer(dst_ids=[ident(c) for c in peers], dma_engine_mask=every, remote_sem=T.sem[s],
+                                              srcs=[a], dsts=[b] * len(peers))], local_sem=T.sem["loc"])
+        total["loc"] += count(every)
+        note("dma", [r], [], "loc", total["loc"])
+
+    def arrives(dst, dw, s, n):
+        total[s] = n
         for e in range(N):
             if e != q:
                 note("dma", [], [R(dst, dw * e, dw * (e + 1))], s, total[s])
@@ -276,13 +295,18 @@ def rank_program(g, core, T, topo):
     S = R("ps0", 120, 128)
     ts(R("emv", 0, 16), R("em16", 0, 16), eF, None, A.is_equal)
     scan(R("pm", 1, 9), S, R("pm", 32, 40), A.max, A.max)
+    ts(qsel, eF, float(q), None, A.is_equal)
     act(R("junk", 0, 8), R("pm", 1, 9), F.Sign, -1.0, R("pm", 8, 9), R("iab", 0, 1))
     ts(R("cm", 0, 8), R("pm", 1, 9), R("pm", 8, 9), BIG, A.is_lt, A.mult)
+    ts(eh, eF, 8.0, 16.0, A.subtract, A.mult)
     tt(R("ab", 0, 8), R("cm", 0, 8), R("pm", 0, 8), A.add)
+    ts(el, eF, 8.0, 2.0, A.subtract, A.mult)
     scan(R("pm", 17, 25), S, R("ab", 0, 8), A.max, A.min)
     act(R("junk", 8, 16), R("pm", 17, 25), F.Sign, -1.0, R("pm", 24, 25), R("iab", 1, 2))
     ts(R("tk", 0, 512, 4), E128, R("iab", 0, 1), None, A.is_equal)
+    ts(flag, pF, float(q), 64.0, A.not_equal, A.mult)
     ts(R("tk", 1, 512, 4), E128, R("iab", 1, 2), None, A.is_equal)
+    ts(R("at", 3, 512, 4), RP, pF, None, A.is_equal)
     qz("tkq", 0, 128, "tk")
 
     k3 = lambda n: R(n, 0, 3)
@@ -310,6 +334,7 @@ def rank_program(g, core, T, topo):
     for b in (2, 3):
         qz("ebq", 128 * b, 128, "eye", 4 - b)
     ts(R("off", 0, 48), R("ps4", 10, 58), 0.5, 64.0, A.mult, A.add)
+    ms(R("at", 512, 528), 0.0)
     act(R("s96", 0, 96), R("s96", 0, 96), F.Copy, -TINY)
     act(R("sc", 9, 12), R("bib", 0, 3), F.Identity, TINY, -0.5 * TINY)
     act(R("tok", 0, 2), R("acc", 0, 2), F.Identity, 0.5, 64.0)
@@ -320,7 +345,7 @@ def rank_program(g, core, T, topo):
         act(R("oa", 128 * k, 128 * k + 128), TI, F.Abs, 1.0, R("nt", k, k + 1))
 
     there = [T.rank_of(c) for c in far]
-    for group in (there[:2], there[2:], [e for e in range(N) if e not in there]):
+    for group in (there[:2], there[2:], [e for e in range(N) if e not in there and e != q]):
         for e in group:
             if e - 1 not in group:
                 n = 1
@@ -329,28 +354,23 @@ def rank_program(g, core, T, topo):
                 pick("sl", 96 * e, 96 * n, "xq", 128, 536, "off", 6 * e)
     out = lambda e: 96 * e
     for to in (far[:2], far[2:], near):
-        send("sl", out, 96, "ld", "arc", True, to)
-    send("sl_s", out, 96, "ld_s", "arp", False, peers)
-    localcopy("sl", 96 * q, "ld", 96 * q, 96, "owc", True)
-    localcopy("sl_s", 96 * q, "ld_s", 96 * q, 96, "owp", False)
+        send("sl", out, 96, "ld", "arc", True, to, wide)
+    send("sl_s", out, 96, "ld_s", "arp", False, peers, thin)
+    pick("ld", 96 * q, 96, "xq", 128, 536, "off", 6 * q)
     localcopy("xq", 256, "rl", 144, 8, "zrc", True)
     localcopy("xq_s", 256, "rl_s", 144, 8, "zrp", False)
-    arrives("ld", 96, "arc")
-    arrives("ld_s", 96, "arp")
+    arrives("ld", 96, "arc", sum(count(m) for m in wide.values()))
+    arrives("ld_s", 96, "arp", sum(count(m) for m in thin.values()))
 
     iota("bt2", 128, [[0, 128]])
-    qz("prq", 0, 128, "prt")
-    ts(R("tri", 0, 512, 4), TI, pF, None, A.is_equal)
-    ts(R("tri", 1, 512, 4), TI, pF, 2.0, A.is_equal, A.mult)
+    act(R("tri", 0, 512, 4), R("eye", 4, 516, 4), F.Copy)
+    act(R("tri", 1, 512, 4), R("eye", 4, 516, 4), F.Copy, 2.0)
     ts(R("o96", 0, 96), R("h96", 0, 96), hF, -BIG, A.not_equal, A.mult)
-    ts(R("at", 3, 512, 4), RP, pF, None, A.is_equal)
-    qz("xq", 0, 128, "tri")
-    ms(R("at", 512, 528), 0.0)
-    ts(flag, pF, float(q), 64.0, A.not_equal, A.mult)
     tt(R("o96", 0, 96), R("o96", 0, 96), R("s96", 0, 96), A.add)
     D16 = R("d16", 0, 12)
     ts(R("blt", 1, 48, 4), D16, e16, 128.0, A.is_equal, A.mult)
     ts(R("blt", 64, 112, 4), D16, e16, iF, A.is_equal, A.mult)
+    qz("xq", 0, 128, "tri")
     mm("ps3", "tkq", 0, "xq", 0, 130)
     for k in range(3):
         act(R("oh", 128 * k, 128 * k + 128), R("oa", 128 * k, 128 * k + 128), F.Relu, -1.0, 1.0)
@@ -367,18 +387,16 @@ def rank_program(g, core, T, topo):
     for k in range(3):
         tt(R("oht", k, 512, 4), R("ps3", 0, 128), R("oh", 128 * k, 128 * k + 128), A.mult)
     qz("uq", 0, 512, "ubb")
-    qz("blq", 0, 144, "blt")
     act(k3("m16"), k3("mm_"), F.Copy, -16.0)
     act(k3("m18"), k3("mm_"), F.Identity, 1.0, -18.0)
-    ts(qsel, eF, float(q), None, A.is_equal)
-    ts(eh, eF, 8.0, 16.0, A.subtract, A.mult)
-    ts(el, eF, 8.0, 2.0, A.subtract, A.mult)
     ts(R("tk", 1, 512, 4), E128, pF, None, A.is_equal)
     ts(R("tk", 0, 512, 4), RP, iF, qsel, A.is_equal, A.mult)
     tt(k3("rr_"), k3("m16"), k3("tok"), A.add)
-    qz("rv", 32, 128, "bv", 128)
-    qz("kq", 0, 128, "tk")
+    for k in range(3):
+        act(R("junk", 128 * k, 128 * k + 128), R("oht", k, 512, 4), F.Copy, acc=R("wk", k, k + 1))
+    act(k3("w18"), k3("wk"), F.Copy, 18.0)
 
+    SG = lambda b, o: R("sg", 384 * (b - 1) + o, 384 * (b - 1) + o + 128)
     MK = lambda b, o: R("mk", 384 * b + o, 384 * b + o + 128)
     pick("xg", 0, 128, "ld", 0, 768, "ofs", 0)
     pick("xg", 128, 128, "ld", 0, 768, "ofs", 8)
@@ -389,15 +407,21 @@ def rank_program(g, core, T, topo):
             mm("ps%d" % i, "wq", 128 * i, "xg", 2 * o, 128)
         for b in range(4):
             mm("ps%d" % (4 + b), "ebq", 128 * b, "xg", 2 * o + 128, 128)
-        for b in (0, 2):
+        nv = 3 - o // 128
+        for b in range(nv):
             ts(MK(b, o), R("ps%d" % b, 0, 128), 0.0, None, A.is_gt)
-        for j, b in enumerate((1, 3)):
-            act(R("sg", 384 * j + o, 384 * j + o + 128), R("ps%d" % b, 0, 128), F.Sign)
-            act(MK(b, o), R("sg", 384 * j + o, 384 * j + o + 128), F.Relu)
+        for b in range(nv, 4):
+            act(SG(b, o), R("ps%d" % b, 0, 128), F.Sign)
+        for b in range(nv, 4):
+            act(MK(b, o), SG(b, o), F.Relu)
         if o == 0:
             picks("xg", 512, 256, "ld", 0, 768, "ofs", 32)
         for b in range(4):
             tt(R("mt", 4 * o + b, 4 * o + 512, 4), R("ps%d" % (4 + b), 0, 128), MK(b, o), A.mult)
+        if o == 0:
+            qz("prq", 0, 128, "prt")
+        if o == 128:
+            qz("blq", 0, 144, "blt")
         qz("mq", o, 128, "mt", 4 * o)
 
     parts = ((0, 256), (256, 128))
@@ -457,13 +481,12 @@ def rank_program(g, core, T, topo):
         ts(R("at", k, 512, 4), RP, rk(k), None, A.is_equal)
     ts(R("at", 516, 528, 4), R("rk", 0, 3), 16.0, None, A.min)
     qz("dxw", 384, 132, "at")
-    ahead = lambda d: 512
-    send("dxw", ahead, 4, "rv", "rkc", True, peers)
-    send("dxw_s", ahead, 4, "rv_s", "rkp", False, peers)
+    spread("dxw", 512, 4, "rv", "rkc", True)
+    spread("dxw_s", 512, 4, "rv_s", "rkp", False)
     localcopy("dxw", 512, "rv", 4 * q, 4, "okc", True)
     localcopy("dxw_s", 512, "rv_s", 4 * q, 4, "okp", False)
-    arrives("rv", 4, "rkc")
-    arrives("rv_s", 4, "rkp")
+    arrives("rv", 4, "rkc", count(every) * len(peers))
+    arrives("rv_s", 4, "rkp", count(every) * len(peers))
     mm("ps2", "dxw", 384, "blq", 0, 128, True, False)
     mm("ps2", "dxw", 384, "blq", 16, 128, False, True)
     shrink("s", 0, 2)
@@ -477,17 +500,16 @@ def rank_program(g, core, T, topo):
     pick("ret", 0, 192, "dxw", 0, 516, "of2", 0)
 
     back = lambda d: 24 * d if d % 2 == 0 else 24 * d + 6
-    send("ret", back, 18, "rl", "rec", True, peers)
-    send("ret_s", back, 18, "rl_s", "rep", False, peers)
+    send("ret", back, 18, "rl", "rec", True, peers, masks)
+    send("ret_s", back, 18, "rl_s", "rep", False, peers, masks)
     localcopy("ret", back(q), "rl", 18 * q, 18, "orc", True)
     localcopy("ret_s", back(q), "rl_s", 18 * q, 18, "orp", False)
-    arrives("rl", 18, "rec")
-    arrives("rl_s", 18, "rep")
+    arrives("rl", 18, "rec", 2 * len(peers))
+    arrives("rl_s", 18, "rep", 2 * len(peers))
     first = 0 if q % 2 == 0 else 2
 
-    for k in range(3):
-        act(R("junk", 128 * k, 128 * k + 128), R("oht", k, 512, 4), F.Copy, acc=R("wk", k, k + 1))
-    act(k3("w18"), k3("wk"), F.Copy, 18.0)
+    qz("rv", 32, 128, "bv", 128)
+    qz("kq", 0, 128, "tk")
     for k in range(3):
         ts(R("aht", 128 + k, 640, 4), RP, R("rr_", k, k + 1), None, A.is_equal)
     tt(k3("cd"), k3("w18"), k3("m18"), A.add)
@@ -503,8 +525,8 @@ def rank_program(g, core, T, topo):
     for k in range(3):
         ts(R("bt2", k, 64, 4), R("cp16", 0, 16), R("cd", k, k + 1), R("rkh", k, k + 1), A.is_equal, A.mult)
     qz("btq", 0, 128, "bt2")
-    mm("ps1", "ahq", 32, "btq", 0, 128, False, True)
     qz("ohq", 0, 128, "oht")
+    mm("ps1", "ahq", 32, "btq", 0, 128, False, True)
     ts(R("of3", 0, 16), R("ps1", 0, 16), 144.0 + first, None, A.add)
 
     for h in range(2):

@@ -3,7 +3,7 @@ from concourse.mybir import dt, AluOpType, AxisListType, ActivationFunctionType
 
 A = AluOpType
 F = ActivationFunctionType
-BIG, FLOOR, TINY, MAGIC16, MAGIC1 = 1e29, -1e25, 2.0 ** -100, 1.5 * 2.0 ** 27, 1.5 * 2.0 ** 23
+BIG, FLOOR, TINY, BELOW, MAGIC16 = 1e29, -1e25, 2.0 ** -120, 1.0 - 2.0 ** -24, 1.5 * 2.0 ** 27
 
 SCRATCH = {}
 ALIAS = {}
@@ -18,34 +18,32 @@ def _mx(name, n):
     _sb(name + "_s", n, "uint8")
 
 
-for _n, _w in (("xq", 664), ("tkq", 128), ("rq", 128), ("sl", 768), ("ld", 768), ("xg", 768), ("wq", 512),
-               ("uq", 512), ("prq", 128), ("ebq", 512), ("mq", 384), ("dxw", 516), ("blq", 144), ("ret", 192), ("rl", 152), ("rv", 160),
-               ("kq", 128), ("ahq", 160), ("ohq", 128), ("btq", 128), ("ctq", 128), ("zc", 256), ("zq", 128)):
+for _n, _w in (("xq", 680), ("lx", 720), ("lg", 720), ("wq", 512), ("uq", 512), ("bq", 160), ("ebq", 512), ("mq", 384), ("dxw", 384),
+               ("atq", 128), ("rl", 384), ("zc", 256), ("zq", 128)):
     _mx(_n, _w)
-for _n, _w in (("xt", 576), ("gt", 544), ("tri", 512), ("tk", 512), ("br", 704), ("wb", 2048), ("ubb", 2048), ("bv", 640),
-               ("pb", 4), ("bp", 640), ("eye", 520), ("mt", 1536), ("dxt", 1536), ("at", 528), ("aht", 640),
-               ("oht", 512), ("zt", 512), ("ti", 128), ("e128", 128), ("rp", 128), ("tmpc", 128), ("oa", 384),
-               ("oh", 384), ("mk", 1536), ("sg", 1152), ("junk", 384), ("dd", 288), ("cmp", 288), ("cc", 288)):
+for _n, _w in (("xt", 576), ("gt", 544), ("tri", 512), ("tk", 512), ("br", 616), ("wb", 2048), ("ubb", 2048), ("bv", 576),
+               ("pb", 4), ("bp", 640), ("mt", 1536), ("dxt", 1536), ("at", 512), ("zt", 512), ("ti", 144), ("e128", 128), ("rp", 128),
+               ("tmpc", 128), ("mk", 1536), ("sg", 384), ("junk", 384), ("cmp", 144), ("rw", 512), ("nz", 128), ("gm", 256), ("gs", 256)):
     _sb(_n, _w, "bfloat16")
-for _n, _w in (("sc", 32), ("pm", 40), ("cm", 16), ("ab", 8), ("iab", 4), ("acc", 4), ("n48", 48), ("ys", 96), ("t96", 96),
-               ("rk", 4), ("tok", 4), ("nt", 4), ("mp", 4), ("mm_", 4), ("m16", 4), ("m18", 4), ("rr_", 4), ("wk", 4), ("w18", 4),
-               ("cd", 4), ("rkh", 4), ("ysb", 128), ("ctsb", 128)):
+for _n, _w in (("sc", 16), ("pm", 40), ("cm", 16), ("ab", 8), ("iab", 4), ("acc", 4), ("n24", 24), ("n16", 16), ("trow", 384), ("st", 4),
+               ("fac", 144), ("th", 144), ("rk", 4), ("cab", 16), ("cum", 4), ("u2", 4), ("e64", 4), ("pos", 4), ("cw", 16), ("ctw", 32),
+               ("ctt", 32), ("ysb", 128)):
     _sb(_n, _w)
 _at = 0
-for _n, _w in (("em16", 16), ("emv", 16), ("g48", 48), ("bi", 16), ("bib", 16), ("d16", 16), ("cp16", 16), ("s96", 96), ("h96", 96),
-               ("o96", 96), ("fx", 48)):
+for _n, _w in (("bi", 4), ("bib", 4), ("ord", 8), ("emv", 8), ("e32", 32), ("l32", 32), ("m32", 32), ("ta", 32), ("tb", 32), ("s48", 48),
+               ("own", 4), ("glf", 4)):
     ALIAS[_n] = ("cs", _at)
     _at += _w
 _sb("cs", _at)
-for _n, _b, _o in (("bt", "br", 0), ("rst", "br", 192), ("blt", "bp", 0), ("prt", "bp", 128), ("bt2", "bv", 0)):
+for _n, _b, _o in (("bt", "br", 0), ("eye", "br", 96), ("blt", "bp", 0), ("prt", "bp", 128)):
     ALIAS[_n] = (_b, _o)
 _sb("pi", 8, "int32")
-for _n, _w in (("off", 48), ("ofs", 48), ("of2", 16), ("of3", 16)):
+for _n, _w in (("off", 24), ("gl", 4), ("of2", 8), ("mo", 16), ("ml", 8), ("pl", 16), ("of3", 16)):
     _sb(_n, _w, "uint16")
 for _k in range(8):
     SCRATCH["ps%d" % _k] = ("psum", [128, 512], "float32")
-SEMAPHORES = ["sv", "ss", "st", "sg", "lx", "lrt", "lgr", "lpr", "lw", "lub", "lv", "arc", "arp", "rec", "rep", "orc", "orp",
-              "rkc", "rkp", "okc", "okp", "zrc", "zrp", "loc", "o_oc", "o_y", "o_ct", "o_s0", "o_s1", "o_s2", "o_s3"]
+SEMAPHORES = ["sv", "ss", "st", "sg", "lx", "lrt", "lgr", "lpr", "lw", "lub", "lv", "axc", "axp", "agc", "agp", "am", "rec", "rep",
+              "loc", "o_oc", "o_y", "o_ct", "o_s0", "o_s1", "o_s2", "o_s3"]
 
 
 def rank_program(g, core, T, topo):
@@ -127,11 +125,17 @@ def rank_program(g, core, T, topo):
         else:
             op("v", rds(in0, s1, s2), [out], lambda: g.vector.tensor_scalar(ap(out), ap(in0), sc_(s1), sc_(s2), op0, op1))
 
-    def tt(out, a, b, o):
-        op("v", [a, b], [out], lambda: g.vector.tensor_tensor(ap(out), ap(a), ap(b), o))
+    def tt(out, a, b, o, by=None):
+        if by is None:
+            op("v", [a, b], [out], lambda: g.vector.tensor_tensor(ap(out), ap(a), ap(b), o))
+        else:
+            op("v", [a, b, by], [out], lambda: g.vector.tensor_tensor(ap(out), ap(a).indirect(ap(by)), ap(b), o))
 
     def cp(out, a):
         op("v", [a], [out], lambda: g.vector.tensor_copy(ap(out), ap(a)))
+
+    def scatter(win, by, a):
+        op("v", [a, by], [win], lambda: g.vector.tensor_copy(ap(win).indirect(ap(by)), ap(a)))
 
     def ms(out, c):
         op("v", [], [out], lambda: g.vector.memset(ap(out), c))
@@ -139,8 +143,8 @@ def rank_program(g, core, T, topo):
     def red(out, a, o):
         op("v", [a], [out], lambda: g.vector.tensor_reduce(ap(out), ap(a), AxisListType.X, o))
 
-    def scan(out, a, z, o0, o1):
-        op("v", [a, z], [out], lambda: g.vector.tensor_tensor_scan(ap(out), ap(a), ap(z), -9e29, o0, o1))
+    def scan(out, a, z, o0, o1, first=-9e29):
+        op("v", [a, z], [out], lambda: g.vector.tensor_tensor_scan(ap(out), ap(a), ap(z), first, o0, o1))
 
     def qz(name, lo, n, tile, t0=0):
         r = R(tile, t0, t0 + 4 * n)
@@ -154,8 +158,8 @@ def rank_program(g, core, T, topo):
             op("s", rds(a, scale, bias), [out, acc],
                lambda: g.scalar.activation(ap(out), ap(a), f, bias=sc_(bias), scale=sc_(scale), accum_out=ap(acc)))
 
-    def zero(name, lane, hi=512, lo=0):
-        act(R(name, lo + lane, hi, 4), R("ti", 0, 128), F.Copy, 0.0)
+    def zero(name, lane):
+        act(R(name, lane, 512, 4), R("ti", 0, 128), F.Copy, 0.0)
 
     def mm(bank, lhs, l0, rhs, r0, n, start=True, stop=True):
         op("t", [R(lhs, l0, l0 + 128), R(lhs + "_s", l0, l0 + 128), R(rhs, r0, r0 + n), R(rhs + "_s", r0, r0 + n)], [R(bank, 0, n)],
@@ -176,63 +180,44 @@ def rank_program(g, core, T, topo):
         pickc(*a)
         picks(*a)
 
-    def iota(name, n, pattern, cm=0):
+    def iota(name, n, pattern, cm=0, base=0):
         r = R(name, 0, n)
-        op("g", [], [r], lambda: g.iota(ap(r), pattern, 0, cm, allow_small_or_imprecise_dtypes=True))
+        op("g", [], [r], lambda: g.iota(ap(r), pattern, base, cm, allow_small_or_imprecise_dtypes=True))
 
     peers = [c for c in T.cores if c != core]
     far = [c for c in peers if topo.die(c) != topo.die(core)]
     mine = [c for c in T.cores if c not in far]
     near = [mine[(mine.index(core) + j) % len(mine)] for j in range(1, len(mine))]
     bits = lambda es: sum(1 << e for e in es)
-    masks = {}
-    for group, first in ((far, 0), (near, 1)):
-        for j, c in enumerate(group):
-            masks[c] = bits(topo.engines(core, c)[first::2][2 * j:2 * j + 2])
-    between = topo.engines(core, near[0])[1::2]
-    wide, thin = dict(masks), dict(masks)
-    wide[near[2]] = bits(between[4:8])
-    thin[near[0]], thin[near[1]], thin[near[2]] = bits(between[0:4]), bits(between[4:6]), bits(between[6:8])
     count = lambda m: bin(m).count("1")
     ident = lambda c: DstId(rid=topo.addr(c)[0], pnc=topo.addr(c)[1])
 
-    def send(src, start, width, dst, s, code, to, use):
-        blocks = [R(src, start(T.rank_of(c)), start(T.rank_of(c)) + width) for c in to]
+    def lanes(side, turn):
+        use = {c: bits(topo.engines(core, c)[side::2][2 * j:2 * j + 2]) for j, c in enumerate(far)}
+        es = topo.engines(core, near[0])[1 - side::2]
+        es = es[4 * turn:] + es[:4 * turn]
+        use[near[0]], use[near[1]], use[near[2]] = bits(es[0:4]), bits(es[4:6]), bits(es[6:8])
+        return use
+
+    place = lambda c, at: [k for k in T.cores if k != at].index(c)
+
+    def send(src, start, width, dst, d0, s, to, use):
+        blocks = [R(src, start(c), start(c) + width) for c in to]
         depend("g", blocks, [])
         ts_ = []
         for c, r in zip(to, blocks):
-            a, b = ap(r), T[dst][:, width * q:width * q + width]
-            if code:
+            at = d0 + width * place(core, c)
+            a, b = ap(r), T[dst][:, at:at + width]
+            if SCRATCH[src][2][-2:] == "x4":
                 a, b = a.bitcast(dt.uint8), b.bitcast(dt.uint8)
             ts_.append(RemoteDMATransfer(dst_ids=[ident(c)], dma_engine_mask=use[c], remote_sem=T.sem[s], src=a, dst=b))
         g.remote_dma_fused(ts_, local_sem=T.sem["loc"])
         total["loc"] = total.get("loc", 0) + sum(count(use[c]) for c in to)
         note("dma", blocks, [], "loc", total["loc"])
 
-    every = topo.mask(core, peers[0])
-
-    def spread(src, start, width, dst, s, code):
-        r = R(src, start, start + width)
-        depend("g", [r], [])
-        a, b = ap(r), T[dst][:, width * q:width * q + width]
-        if code:
-            a, b = a.bitcast(dt.uint8), b.bitcast(dt.uint8)
-        g.remote_dma_fused([RemoteDMATransfer(dst_ids=[ident(c) for c in peers], dma_engine_mask=every, remote_sem=T.sem[s],
-                                              srcs=[a], dsts=[b] * len(peers))], local_sem=T.sem["loc"])
-        total["loc"] += count(every)
-        note("dma", [r], [], "loc", total["loc"])
-
-    def arrives(dst, dw, s, n):
-        total[s] = n
-        for e in range(N):
-            if e != q:
-                note("dma", [], [R(dst, dw * e, dw * (e + 1))], s, total[s])
-
-    def localcopy(src, a, dst, b, width, s, code):
-        i, o = T[src][:, a:a + width], T[dst][:, b:b + width]
-        if code:
-            i, o = i.bitcast(dt.uint8), o.bitcast(dt.uint8)
-        dma("y", [R(src, a, a + width)], [R(dst, b, b + width)], o, i, s)
+    def arrives(dst, d0, width, s):
+        total[s] = sum(count(m) for m in lanes(0, 0).values())
+        note("dma", [], [R(dst, d0, d0 + width * len(peers))], s, total[s])
 
     def load(qn, name, w, src, s, at=0):
         r = R(name, at, at + w)
@@ -244,23 +229,19 @@ def rank_program(g, core, T, topo):
     load("s", "pb", 4, T.pr[:, 0:4], "lpr")
     load("y", "wb", 2048, T.w[:, :], "lw")
     load("s", "ubb", 2048, T.ub[:, :], "lub")
-    load("y", "bv", 512, T.v[:, :], "lv", 128)
+    load("y", "bv", 512, T.v[:, :], "lv", 64)
 
     iota("pi", 1, [[1, 1]], cm=1)
-    iota("ti", 128, [[1, 128]])
+    iota("ti", 144, [[1, 144]])
     iota("rp", 128, [[0, 8], [1, 16]])
     iota("bi", 3, [[16, 3]])
-    iota("em16", 16, [[1, 8], [0, 2]])
-    iota("g48", 48, [[1, 8], [100, 2], [0, 3]])
     iota("e128", 128, [[1, 8], [0, 16]])
-    iota("fx", 48, [[16, 3], [48, 2], [96, 8]])
-    iota("d16", 12, [[32, 4], [8, 3]])
-    iota("s96", 96, [[16, 3], [0, 2], [1, 16]])
-    iota("h96", 96, [[0, 3], [1, 2], [0, 16]])
-    iota("cp16", 16, [[18, 2], [1, 8]])
-    iota("blt", 128, [[0, 128]])
+    iota("e32", 32, [[1, 8], [0, 4]])
+    iota("l32", 32, [[0, 8], [1, 4]])
+    iota("s48", 48, [[1, 3], [3, 16]])
+    iota("glf", 3, [[128, 3]], cm=1)
     col = lambda k: R("sc", k, k + 1)
-    pF, iF, eF, hF, e100, iH, flag, e16, eh, el, qsel = [col(k) for k in (0, 1, 2, 3, 5, 6, 7, 8, 12, 13, 14)]
+    pF, iF, eF, iH, e16, negi, i4, i3 = [col(k) for k in range(8)]
     TI, RP, E128 = R("ti", 0, 128), R("rp", 0, 128), R("e128", 0, 128)
     p0 = R("pi", 0, 1)
     ms(R("xt", 512, 544), 0.0)
@@ -268,164 +249,139 @@ def rank_program(g, core, T, topo):
     ms(R("gt", 512, 544), 0.0)
     ts(R("pi", 1, 2), p0, 15, None, A.bitwise_and)
     ts(R("pi", 2, 3), p0, 4, None, A.arith_shift_right)
-    ts(R("pi", 3, 4), p0, 4, 1, A.arith_shift_right, A.bitwise_and)
-    ms(R("eye", 0, 520), 0.0)
-    cp(R("sc", 0, 4), R("pi", 0, 4))
+    ms(R("br", 0, 616), 0.0)
+    cp(R("sc", 0, 3), R("pi", 0, 3))
+    ms(R("bv", 0, 64), 0.0)
+    ms(R("ctw", 0, 32), 0.0)
     ts(R("eye", 4, 516, 4), TI, pF, None, A.is_equal)
-    for lane in range(4):
+    for lane in (0, 1):
         ts(R("tri", lane, 512, 4), TI, pF, None, A.is_ge)
-    for lane in range(4):
-        ts(R("rst", lane, 512, 4), RP, iF, None, A.is_equal)
+    for lane in (2, 3):
+        ts(R("tri", lane, 512, 4), RP, iF, None, A.is_equal)
     zero("tk", 2)
     zero("tk", 3)
-    zero("oht", 3)
-    zero("aht", 3, 640, 128)
-    act(R("aht", 0, 128), TI, F.Copy, 0.0)
-    act(e100, eF, F.Identity, 1.0, 100.0)
     act(iH, iF, F.Identity, 1.0, 0.5)
-    act(e16, eF, F.Copy, 16.0)
     act(R("bib", 0, 3), R("bi", 0, 3), F.Identity, 1.0, iH)
-    qz("xq", 128, 144, "xt")
-    mm("ps0", "xq", 128, "xq", 144, 128)
-    qz("xq", 272, 128, "tri")
+    order = [T.rank_of(c) for c in [core] + sorted(near) + far]
+    m = 0
+    while m < N:
+        n = 1
+        while m + n < N and order[m + n] == order[m] + n:
+            n += 1
+        act(R("ord", m, m + n), R("ti", order[m], order[m] + n), F.Copy)
+        m += n
+    zero("at", 3)
+    qz("xq", 0, 144, "xt")
+    mm("ps0", "xq", 0, "xq", 16, 128)
+    qz("xq", 144, 128, "tri")
     qz("ebq", 0, 128, "eye", 4)
-    ts(R("bt", 2, 192, 4), R("g48", 0, 48), e100, 512.0, A.is_equal, A.mult)
-    act(R("bt", 3, 192, 4), R("bt", 2, 192, 4), F.Copy, 0.0625)
 
     S = R("ps0", 120, 128)
-    ts(R("emv", 0, 16), R("em16", 0, 16), eF, None, A.is_equal)
     scan(R("pm", 1, 9), S, R("pm", 32, 40), A.max, A.max)
-    ts(qsel, eF, float(q), None, A.is_equal)
+    ts(R("emv", 0, 8), R("ord", 0, 8), eF, None, A.is_equal)
     act(R("junk", 0, 8), R("pm", 1, 9), F.Sign, -1.0, R("pm", 8, 9), R("iab", 0, 1))
     ts(R("cm", 0, 8), R("pm", 1, 9), R("pm", 8, 9), BIG, A.is_lt, A.mult)
-    ts(eh, eF, 8.0, 16.0, A.subtract, A.mult)
+    ts(R("m32", 0, 32), R("e32", 0, 32), eF, None, A.is_equal)
     tt(R("ab", 0, 8), R("cm", 0, 8), R("pm", 0, 8), A.add)
-    ts(el, eF, 8.0, 2.0, A.subtract, A.mult)
+    ts(R("nz", 0, 128), RP, 0.5, None, A.is_gt)
     scan(R("pm", 17, 25), S, R("ab", 0, 8), A.max, A.min)
     act(R("junk", 8, 16), R("pm", 17, 25), F.Sign, -1.0, R("pm", 24, 25), R("iab", 1, 2))
     ts(R("tk", 0, 512, 4), E128, R("iab", 0, 1), None, A.is_equal)
-    ts(flag, pF, float(q), 64.0, A.not_equal, A.mult)
-    ts(R("tk", 1, 512, 4), E128, R("iab", 1, 2), None, A.is_equal)
-    ts(R("at", 3, 512, 4), RP, pF, None, A.is_equal)
-    qz("tkq", 0, 128, "tk")
-
-    k3 = lambda n: R(n, 0, 3)
-    mm("ps1", "tkq", 0, "xq", 270, 130)
-    mm("ps2", "tkq", 0, "xq", 270, 130)
-    qz("rq", 0, 128, "rst")
-    qz("xq", 400, 136, "gt")
     qz("ebq", 128, 128, "eye", 3)
+    ts(R("tk", 1, 512, 4), E128, R("iab", 1, 2), None, A.is_equal)
+    cp(R("gl", 0, 3), R("glf", 0, 3))
+    qz("xq", 288, 128, "tk")
+
+    mm("ps1", "xq", 288, "xq", 142, 130)
+    mm("ps2", "xq", 288, "xq", 142, 130)
+    qz("xq", 416, 136, "gt")
+    qz("ebq", 256, 128, "eye", 2)
     for k in range(2):
         act(R("junk", 16 + 128 * k, 144 + 128 * k), R("ps1", 2, 130), F.Sign, -1.0, R("bib", k, k + 1), R("acc", k, k + 1))
     ts(R("tmpc", 0, 128), R("ps2", 2, 130), R("bib", 2, 3), 0.5, A.is_lt, A.subtract)
-    ts(R("ofs", 0, 48), R("fx", 0, 48), iF, None, A.add)
+    act(e16, eF, F.Identity, 16.0, -128.0)
     red(R("acc", 2, 3), R("tmpc", 0, 128), A.add)
+    mm("ps3", "xq", 144, "xq", 288, 130)
     for k in range(2):
-        act(R("n48", k, 48, 3), R("emv", 0, 16), F.Copy, R("acc", k, k + 1))
-    ts(R("prt", 0, 512, 4), TI, 0.0, R("pb", 0, 1), A.mult, A.add)
-    ts(R("n48", 2, 48, 3), R("emv", 0, 16), R("acc", 2, 3), 2.0, A.mult, A.mult)
-    ts(R("prt", 1, 512, 4), TI, 0.0, R("pb", 1, 2), A.mult, A.add)
-    ts(R("bt", 0, 192, 4), R("n48", 0, 48), MAGIC16, MAGIC16, A.add, A.subtract)
-    ts(R("prt", 2, 512, 4), TI, 0.0, R("pb", 2, 3), A.mult, A.add)
-    tt(R("bt", 1, 192, 4), R("n48", 0, 48), R("bt", 0, 192, 4), A.subtract)
-    ts(R("prt", 3, 512, 4), TI, 0.0, R("pb", 3, 4), A.mult, A.add)
-    qz("xq", 536, 128, "bt")
-    mm("ps4", "rq", 0, "xq", 526, 128)
-    for b in (2, 3):
-        qz("ebq", 128 * b, 128, "eye", 4 - b)
-    ts(R("off", 0, 48), R("ps4", 10, 58), 0.5, 64.0, A.mult, A.add)
-    ms(R("at", 512, 528), 0.0)
-    act(R("s96", 0, 96), R("s96", 0, 96), F.Copy, -TINY)
-    act(R("sc", 9, 12), R("bib", 0, 3), F.Identity, TINY, -0.5 * TINY)
-    act(R("tok", 0, 2), R("acc", 0, 2), F.Identity, 0.5, 64.0)
-    act(R("tok", 2, 3), R("acc", 2, 3), F.Identity, 1.0, 64.0)
-    act(k3("nt"), k3("tok"), F.Copy, -1.0)
-    act(k3("mp"), k3("tok"), F.Identity, 0.0625, -0.46875)
-    for k in range(3):
-        act(R("oa", 128 * k, 128 * k + 128), TI, F.Abs, 1.0, R("nt", k, k + 1))
+        act(R("n24", k, 24, 3), R("emv", 0, 8), F.Copy, R("acc", k, k + 1))
+    ts(R("n24", 2, 24, 3), R("emv", 0, 8), R("acc", 2, 3), 2.0, A.mult, A.mult)
+    tt(R("cab", 0, 8), R("ps3", 0, 128, 16), R("tk", 0, 512, 64), A.mult)
+    ts(R("bt", 2, 96, 4), R("n24", 0, 24), MAGIC16, MAGIC16, A.add, A.subtract)
+    tt(R("cab", 8, 16), R("ps3", 0, 128, 16), R("tk", 1, 512, 64), A.mult)
+    tt(R("bt", 3, 96, 4), R("n24", 0, 24), R("bt", 2, 96, 4), A.subtract)
+    red(R("cum", 0, 1), R("cab", 0, 8), A.add)
+    qz("xq", 552, 128, "bt")
+    mm("ps4", "xq", 144, "xq", 542, 128)
+    red(R("cum", 1, 2), R("cab", 8, 16), A.add)
+    qz("ebq", 384, 128, "eye", 1)
+    ts(R("off", 0, 24), R("ps4", 10, 34), 0.5, 64.0, A.mult, A.add)
+    act(negi, iF, F.Copy, -1.0)
+    act(i4, iF, F.Copy, 4.0)
+    act(i3, iF, F.Copy, 3.0)
+    act(R("e64", 0, 2), R("iab", 0, 2), F.Copy, 64.0)
+    ts(R("u2", 0, 2), R("cum", 0, 2), 49.0, -257.0, A.min, A.add)
 
-    there = [T.rank_of(c) for c in far]
-    for group in (there[:2], there[2:], [e for e in range(N) if e not in there and e != q]):
-        for e in group:
-            if e - 1 not in group:
-                n = 1
-                while e + n in group:
-                    n += 1
-                pick("sl", 96 * e, 96 * n, "xq", 128, 536, "off", 6 * e)
-    out = lambda e: 96 * e
-    for to in (far[:2], far[2:], near):
-        send("sl", out, 96, "ld", "arc", True, to, wide)
-    send("sl_s", out, 96, "ld_s", "arp", False, peers, thin)
-    pick("ld", 96 * q, 96, "xq", 128, 536, "off", 6 * q)
-    localcopy("xq", 256, "rl", 144, 8, "zrc", True)
-    localcopy("xq_s", 256, "rl_s", 144, 8, "zrp", False)
-    arrives("ld", 96, "arc", sum(count(m) for m in wide.values()))
-    arrives("ld_s", 96, "arp", sum(count(m) for m in thin.values()))
+    out = lambda c: 336 + 48 * order.index(T.rank_of(c))
+    pick("lx", 528, 192, "xq", 0, 144, "off", 12)
+    pick("lx", 336, 192, "xq", 0, 144, "off", 0)
+    pick("lg", 336, 384, "xq", 416, 552, "off", 0)
+    send("lx", out, 48, "lx", 0, "axc", far, lanes(0, 0))
+    send("lx", out, 48, "lx", 0, "axc", near, lanes(0, 0))
+    send("lx_s", out, 48, "lx_s", 0, "axp", peers, lanes(1, 0))
+    send("lg", out, 48, "lg", 0, "agc", peers, lanes(1, 1))
+    send("lg_s", out, 48, "lg_s", 0, "agp", peers, lanes(0, 1))
+    for name, s in (("lx", "axc"), ("lx_s", "axp"), ("lg", "agc"), ("lg_s", "agp")):
+        arrives(name, 0, 48, s)
 
-    iota("bt2", 128, [[0, 128]])
-    act(R("tri", 0, 512, 4), R("eye", 4, 516, 4), F.Copy)
-    act(R("tri", 1, 512, 4), R("eye", 4, 516, 4), F.Copy, 2.0)
-    ts(R("o96", 0, 96), R("h96", 0, 96), hF, -BIG, A.not_equal, A.mult)
-    tt(R("o96", 0, 96), R("o96", 0, 96), R("s96", 0, 96), A.add)
-    D16 = R("d16", 0, 12)
-    ts(R("blt", 1, 48, 4), D16, e16, 128.0, A.is_equal, A.mult)
-    ts(R("blt", 64, 112, 4), D16, e16, iF, A.is_equal, A.mult)
-    qz("xq", 0, 128, "tri")
-    mm("ps3", "tkq", 0, "xq", 0, 130)
-    for k in range(3):
-        act(R("oh", 128 * k, 128 * k + 128), R("oa", 128 * k, 128 * k + 128), F.Relu, -1.0, 1.0)
-    act(R("blt", 2, 48, 4), R("blt", 1, 48, 4), F.Copy, 2.0)
-    act(R("blt", 3, 48, 4), D16, F.Copy)
-    for k in (1, 2):
-        act(R("blt", 64 + k, 112, 4), R("blt", 64, 112, 4), F.Copy)
-    act(R("at", 517, 528, 4), R("ti", 0, 3), F.Identity, 0.0, flag)
-    for k in range(3):
-        act(R("cc", 96 * k, 96 * k + 96), R("o96", 0, 96), F.Identity, 1.0, col(9 + k))
+    iota("rw", 512, [[0, 512]], base=144)
     qz("wq", 0, 512, "wb")
-    ms(R("blt", 7, 48, 12), 512.0)
-    ts(k3("mm_"), k3("mp"), MAGIC1, MAGIC1, A.add, A.subtract)
+    tt(R("pos", 0, 2), R("u2", 0, 2), R("e64", 0, 2), A.add)
+    for k in range(2):
+        act(R("n16", 8 * k, 8 * k + 8), R("m32", 0, 32, 4), F.Copy, R("pos", k, k + 1))
+    act(R("ta", 0, 32), R("l32", 0, 32), F.Identity, 128.0, e16)
+    act(R("tb", 0, 32), R("l32", 0, 32), F.Identity, 1.0, negi)
+    act(R("own", 0, 3), R("ti", 0, 3), F.Identity, 1.0, i3)
+    act(R("blt", 32, 64), R("m32", 0, 32), F.Copy, i4)
+    act(R("blt", 64, 96), R("m32", 0, 32), F.Copy, iF)
+    for lane in range(4):
+        act(R("prt", lane, 512, 4), TI, F.Identity, 0.0, R("pb", lane, lane + 1))
+    qz("rl", 240, 144, "bv")
+    ts(R("bt", 2, 64, 4), R("n16", 0, 16), MAGIC16, MAGIC16, A.add, A.subtract)
+    tt(R("blt", 0, 32), R("ta", 0, 32), R("m32", 0, 32), A.mult)
+    tt(R("bt", 3, 64, 4), R("n16", 0, 16), R("bt", 2, 64, 4), A.subtract)
+    tt(R("blt", 96, 128), R("tb", 0, 32), R("m32", 0, 32), A.mult)
+    qz("xq", 552, 128, "bt")
+    mm("ps4", "xq", 144, "xq", 542, 128)
     for k in range(3):
-        tt(R("oht", k, 512, 4), R("ps3", 0, 128), R("oh", 128 * k, 128 * k + 128), A.mult)
+        ts(R("fac", 48 * k, 48 * k + 48), R("s48", 0, 48), R("own", k, k + 1), BELOW, A.is_ge, A.max)
+    ts(R("pl", 0, 16), R("ps4", 10, 26), 256.0, None, A.add)
     qz("uq", 0, 512, "ubb")
-    act(k3("m16"), k3("mm_"), F.Copy, -16.0)
-    act(k3("m18"), k3("mm_"), F.Identity, 1.0, -18.0)
-    ts(R("tk", 1, 512, 4), E128, pF, None, A.is_equal)
-    ts(R("tk", 0, 512, 4), RP, iF, qsel, A.is_equal, A.mult)
-    tt(k3("rr_"), k3("m16"), k3("tok"), A.add)
-    for k in range(3):
-        act(R("junk", 128 * k, 128 * k + 128), R("oht", k, 512, 4), F.Copy, acc=R("wk", k, k + 1))
-    act(k3("w18"), k3("wk"), F.Copy, 18.0)
+    qz("bq", 0, 160, "bp")
 
-    SG = lambda b, o: R("sg", 384 * (b - 1) + o, 384 * (b - 1) + o + 128)
-    MK = lambda b, o: R("mk", 384 * b + o, 384 * b + o + 128)
-    pick("xg", 0, 128, "ld", 0, 768, "ofs", 0)
-    pick("xg", 128, 128, "ld", 0, 768, "ofs", 8)
-    pick("xg", 256, 256, "ld", 0, 768, "ofs", 16)
-    pickc("xg", 512, 256, "ld", 0, 768, "ofs", 32)
-    for o in (0, 128, 256):
-        for i in range(4):
-            mm("ps%d" % i, "wq", 128 * i, "xg", 2 * o, 128)
-        for b in range(4):
-            mm("ps%d" % (4 + b), "ebq", 128 * b, "xg", 2 * o + 128, 128)
-        nv = 3 - o // 128
-        for b in range(nv):
-            ts(MK(b, o), R("ps%d" % b, 0, 128), 0.0, None, A.is_gt)
-        for b in range(nv, 4):
-            act(SG(b, o), R("ps%d" % b, 0, 128), F.Sign)
-        for b in range(nv, 4):
-            act(MK(b, o), SG(b, o), F.Relu)
-        if o == 0:
-            picks("xg", 512, 256, "ld", 0, 768, "ofs", 32)
-        for b in range(4):
-            tt(R("mt", 4 * o + b, 4 * o + 512, 4), R("ps%d" % (4 + b), 0, 128), MK(b, o), A.mult)
-        if o == 0:
-            qz("prq", 0, 128, "prt")
-        if o == 128:
-            qz("blq", 0, 144, "blt")
-        qz("mq", o, 128, "mt", 4 * o)
+    MK = lambda b: R("mk", 384 * b, 384 * b + 384)
+    for i in range(4):
+        mm("ps%d" % i, "wq", 128 * i, "lx", 0, 384)
+    act(R("sg", 0, 384), R("ps0", 0, 384), F.Sign)
+    act(MK(0), R("sg", 0, 384), F.Relu)
+    for b in (1, 2, 3):
+        ts(MK(b), R("ps%d" % b, 0, 384), 0.0, None, A.is_gt)
+    for b in range(4):
+        mm("ps%d" % (4 + b), "ebq", 128 * b, "lg", 0, 384)
+
+    def masked(k, b):
+        tt(R("mt", 512 * k + b, 512 * k + 512, 4), R("ps%d" % (4 + b), k, 384, 3), R("mk", 384 * b + k, 384 * b + 384, 3), A.mult)
+
+    for b in range(4):
+        masked(0, b)
+        masked(1, b)
+    masked(2, 0)
+    qz("mq", 0, 256, "mt")
+    for b in (1, 2, 3):
+        masked(2, b)
+    qz("mq", 256, 128, "mt", 1024)
 
     parts = ((0, 256), (256, 128))
-    UB = (("ps2", "ps3", "ps5", "ps6"), ("ps7", "ps0", "ps1", "ps4"))
+    UB = (("ps3", "ps0", "ps1", "ps2"), ("ps6", "ps7", "ps4", "ps5"))
 
     def product(h, i):
         mm(UB[h][i], "uq", 128 * i, "mq", parts[h][0], parts[h][1])
@@ -437,116 +393,85 @@ def rank_program(g, core, T, topo):
         else:
             ts(R("dxt", 4 * o + i, 4 * (o + n), 4), R(UB[h][i], 0, n), 0.0625, None, A.mult)
 
-    D = lambda k, a, b: R("dd", 96 * k + a, 96 * k + b)
-    C = lambda k, a, b: R("cmp", 96 * k + a, 96 * k + b)
-    CC = lambda k, a, b: R("cc", 96 * k + a, 96 * k + b)
-    st = lambda k: R("ys", 32 * k, 32 * k + 1)
-    rk = lambda k: R("rk", k, k + 1)
-
-    def turn(a, b):
-        op("v", [R("ys", a, b)], [R("t96", a, b)], lambda: g.vector.transpose(T.t96[:, a:b], T.ys[:, a:b]))
-
-    def less(k, a, b):
-        act(D(k, a, b), R("t96", a, b), F.Identity, -1.0, st(k))
-
+    st = lambda k: R("st", k, k + 1)
+    w48 = lambda name, k: R(name, 48 * k, 48 * k + 48)
     for k in (0, 1):
-        mm("ps%d" % k, "mq", 128 * k, "prq", 0, 128)
+        mm("ps%d" % k, "mq", 128 * k, "bq", 32, 128)
+    mm("ps2", "bq", 32, "mq", 0, 256)
     product(0, 0)
     for k in (0, 1):
-        act(R("ys", 32 * k, 32 * k + 32), R("ps%d" % k, 0, 32), F.Abs)
-    mm("ps4", "mq", 256, "prq", 0, 128)
-    for i in (1, 2, 3):
-        product(0, i)
-    turn(0, 64)
-    shrink("v", 0, 0)
+        act(st(k), R("ps%d" % k, 0, 1), F.Abs, 1.0, TINY)
+    act(R("trow", 0, 256), R("ps2", 0, 256), F.Abs, 1.0, TINY)
+    product(0, 1)
+    product(0, 2)
+    mm("ps4", "bq", 32, "mq", 256, 128)
+    mm("ps5", "mq", 256, "bq", 32, 128)
+    product(0, 3)
     for k in (0, 1):
-        less(k, 0, 64)
-    tt(C(0, 0, 64), D(0, 0, 64), CC(0, 0, 64), A.is_lt)
-    act(R("ys", 64, 96), R("ps4", 0, 32), F.Abs)
+        act(w48("th", k), w48("fac", k), F.Copy, st(k))
+    act(R("trow", 256, 384), R("ps4", 0, 128), F.Abs, 1.0, TINY)
+    act(st(2), R("ps5", 0, 1), F.Abs, 1.0, TINY)
+    act(w48("th", 2), w48("fac", 2), F.Copy, st(2))
     for i in range(4):
         product(1, i)
-    turn(64, 96)
-    for k in (0, 1):
-        less(k, 64, 96)
-    ts(D(2, 0, 96), R("t96", 0, 96), st(2), -1.0, A.subtract, A.mult)
-    tt(C(1, 0, 64), D(1, 0, 64), CC(1, 0, 64), A.is_lt)
-    for k in (0, 1):
-        tt(C(k, 64, 96), D(k, 64, 96), CC(k, 64, 96), A.is_lt)
-    tt(C(2, 0, 96), D(2, 0, 96), CC(2, 0, 96), A.is_lt)
-    shrink("s", 0, 1)
-    for k in (0, 1):
-        act(R("junk", 96 * k, 96 * k + 96), C(k, 0, 96), F.Copy, acc=rk(k))
-    red(rk(2), C(2, 0, 96), A.add)
-    for k in (0, 1, 2):
-        ts(R("at", k, 512, 4), RP, rk(k), None, A.is_equal)
-    ts(R("at", 516, 528, 4), R("rk", 0, 3), 16.0, None, A.min)
-    qz("dxw", 384, 132, "at")
-    spread("dxw", 512, 4, "rv", "rkc", True)
-    spread("dxw_s", 512, 4, "rv_s", "rkp", False)
-    localcopy("dxw", 512, "rv", 4 * q, 4, "okc", True)
-    localcopy("dxw_s", 512, "rv_s", 4 * q, 4, "okp", False)
-    arrives("rv", 4, "rkc", count(every) * len(peers))
-    arrives("rv_s", 4, "rkp", count(every) * len(peers))
-    mm("ps2", "dxw", 384, "blq", 0, 128, True, False)
-    mm("ps2", "dxw", 384, "blq", 16, 128, False, True)
+    shrink("v", 0, 0)
+    shrink("v", 0, 1)
     shrink("s", 0, 2)
     shrink("s", 0, 3)
-    qz("dxw", 0, 256, "dxt")
-    for i in range(3):
+    for k in range(3):
+        tt(w48("cmp", k), R("trow", 0, 384), w48("th", k), A.is_gt, R("gl", 0, 3))
+    for k in range(3):
+        red(R("rk", k, k + 1), w48("cmp", k), A.add)
+    for k in range(3):
+        ts(R("at", k, 512, 4), RP, R("rk", k, k + 1), None, A.is_equal)
+    qz("atq", 0, 128, "at")
+    mm("ps3", "atq", 0, "bq", 0, 128, True, False)
+    mm("ps3", "atq", 0, "bq", 16, 128, False, True)
+    for i in range(4):
         shrink("s", 1, i)
-    shrink("v", 1, 3)
+    qz("dxw", 0, 256, "dxt")
+    ts(R("mo", 0, 16, 2), R("ps3", 8, 16), 64.0 * q, None, A.add)
+    ts(R("of2", 0, 8), R("ps3", 0, 8), 128.0, None, A.add)
     qz("dxw", 256, 128, "dxt", 1024)
-    cp(R("of2", 0, 12), R("ps2", 0, 12))
-    pick("ret", 0, 192, "dxw", 0, 516, "of2", 0)
+    pick("rl", 0, 128, "dxw", 0, 384, "of2", 0)
 
-    back = lambda d: 24 * d if d % 2 == 0 else 24 * d + 6
-    send("ret", back, 18, "rl", "rec", True, peers, masks)
-    send("ret_s", back, 18, "rl_s", "rep", False, peers, masks)
-    localcopy("ret", back(q), "rl", 18 * q, 18, "orc", True)
-    localcopy("ret_s", back(q), "rl_s", 18 * q, 18, "orp", False)
-    arrives("rl", 18, "rec", 2 * len(peers))
-    arrives("rl_s", 18, "rep", 2 * len(peers))
-    first = 0 if q % 2 == 0 else 2
+    send("mo", lambda c: 2 * place(c, core), 1, "ml", 0, "am", peers, lanes(0, 0))
+    send("rl", lambda c: 16 * place(c, core), 16, "rl", 128, "rec", peers, lanes(1, 0))
+    send("rl_s", lambda c: 16 * place(c, core), 16, "rl_s", 128, "rep", peers, lanes(0, 1))
+    arrives("ml", 0, 1, "am")
+    arrives("rl", 128, 16, "rec")
+    arrives("rl_s", 128, 16, "rep")
 
-    qz("rv", 32, 128, "bv", 128)
-    qz("kq", 0, 128, "tk")
-    for k in range(3):
-        ts(R("aht", 128 + k, 640, 4), RP, R("rr_", k, k + 1), None, A.is_equal)
-    tt(k3("cd"), k3("w18"), k3("m18"), A.add)
-    for k in range(3):
-        ts(R("aht", k, 64, 4), R("cp16", 0, 16), R("cd", k, k + 1), eh, A.is_equal, A.mult)
-        ts(R("aht", 64 + k, 128, 4), R("cp16", 0, 16), R("cd", k, k + 1), el, A.is_equal, A.mult)
-    qz("ahq", 0, 160, "aht")
-    mm("ps0", "kq", 0, "rv", 0, 128)
-    mm("ps1", "ahq", 32, "ahq", 0, 128, True, False)
-    mm("ps1", "ahq", 32, "ahq", 16, 128, False, False)
-    for k in range(3):
-        red(R("rkh", k, k + 1), R("ps0", 1 + k, 32, 4), A.min)
-    for k in range(3):
-        ts(R("bt2", k, 64, 4), R("cp16", 0, 16), R("cd", k, k + 1), R("rkh", k, k + 1), A.is_equal, A.mult)
-    qz("btq", 0, 128, "bt2")
-    qz("ohq", 0, 128, "oht")
-    mm("ps1", "ahq", 32, "btq", 0, 128, False, True)
-    ts(R("of3", 0, 16), R("ps1", 0, 16), 144.0 + first, None, A.add)
+    RW = R("rw", 0, 512)
+    h128 = lambda name, h: R(name, 128 * h, 128 * h + 128)
+    ends = lambda h: R("gs", 128 * h + 15, 128 * h + 128, 16)
+    scatter(RW, R("mo", 14, 15), R("ti", 16, 32))
+    scatter(RW, R("ml", 0, 7), R("ti", 32, 144))
+    for h in range(2):
+        tt(h128("gm", h), RW, R("tri", 2, 512, 4), A.mult, R("pl", 8 * h, 8 * h + 8))
+    for h in range(2):
+        scan(h128("gs", h), R("nz", 0, 128), h128("gm", h), A.mult, A.add, 0.0)
+    for h in range(2):
+        cp(R("of3", 8 * h, 8 * h + 8), ends(h))
 
     for h in range(2):
-        pick("zc", 128 * h, 128, "rl", 0, 152, "of3", 8 * h)
+        pick("zc", 128 * h, 128, "rl", 96, 256, "of3", 8 * h)
         for b in range(4):
             mm("ps%d" % (4 + b), "ebq", 128 * b, "zc", 128 * h, 128, h == 0, h == 1)
-    ts(R("bt2", 64, 67), k3("rkh"), 15.5, None, A.is_lt)
-    qz("ctq", 0, 128, "bt2")
-    mm("ps2", "ctq", 0, "ohq", 0, 128)
+    for h in range(2):
+        ts(R("cw", 8 * h, 8 * h + 8), ends(h), 143.5, 1.0 + h, A.is_lt, A.mult)
+    tt(R("ctw", 0, 8), R("cw", 0, 8), R("cw", 8, 16), A.add)
+    op("v", [R("ctw", 0, 32)], [R("ctt", 0, 32)], lambda: g.vector.transpose(T.ctt[0:32, 0:32], T.ctw[0:32, 0:32]))
+    dma("y", [R("ctt", 0, 32)], [], T.ct[:, :], T.ctt[0:8, 0:16], "o_ct")
     for b in (0, 2):
         act(R("zt", b, 512, 4), R("ps%d" % (4 + b), 0, 128), F.Copy)
     for b in (1, 3):
         cp(R("zt", b, 512, 4), R("ps%d" % (4 + b), 0, 128))
     qz("zq", 0, 128, "zt")
-    mm("ps3", "rv", 32, "zq", 0, 128)
-    act(R("ctsb", 0, 128), R("ps2", 0, 128), F.Copy)
+    mm("ps3", "rl", 256, "zq", 0, 128)
     dma("y", [R("zq", 0, 128)], [], T.oc[:, :], T.zq[:, 0:128].bitcast(dt.uint8), "o_oc")
     for k in range(4):
         dma("y" if k < 1 else "s", [R("zq_s", 0, 128)], [], T.osc[4 * k:4 * k + 4, 0:128], T.zq_s[32 * k:32 * k + 4, 0:128], "o_s%d" % k)
-    dma("s", [R("ctsb", 0, 128)], [], T.ct[:, :], T.ctsb[16:17, 0:128], "o_ct")
     cp(R("ysb", 0, 128), R("ps3", 0, 128))
     dma("y", [R("ysb", 0, 128)], [], T.y[:, :], T.ysb[:, 0:128], "o_y")
 

from concourse.bass import DstId, RemoteDMATransfer
from concourse.mybir import dt, AluOpType, AxisListType, ActivationFunctionType

A = AluOpType
F = ActivationFunctionType
BIG, FLOOR, TINY, BELOW, MAGIC16 = 1e29, -1e25, 2.0 ** -120, 1.0 - 2.0 ** -24, 1.5 * 2.0 ** 27

SCRATCH = {}
ALIAS = {}


def _sb(name, n, d="float32"):
    SCRATCH[name] = ("sbuf", [128, n], d)


def _mx(name, n):
    _sb(name, n, "float8_e4m3fn_x4")
    _sb(name + "_s", n, "uint8")


for _n, _w in (("xq", 680), ("lx", 720), ("lg", 720), ("wq", 512), ("uq", 512), ("bq", 160), ("ebq", 512), ("mq", 384), ("dxw", 384),
               ("atq", 128), ("rl", 384), ("zc", 256), ("zq", 128)):
    _mx(_n, _w)
for _n, _w in (("xt", 576), ("gt", 544), ("tri", 512), ("tk", 512), ("br", 616), ("wb", 2048), ("ubb", 2048), ("bv", 576),
               ("pb", 4), ("bp", 640), ("mt", 1536), ("dxt", 1536), ("at", 512), ("zt", 512), ("ti", 144), ("e128", 128), ("rp", 128),
               ("tmpc", 128), ("mk", 1536), ("sg", 384), ("junk", 384), ("cmp", 144), ("rw", 512), ("nz", 128), ("gm", 256), ("gs", 256)):
    _sb(_n, _w, "bfloat16")
for _n, _w in (("sc", 16), ("pm", 40), ("cm", 16), ("ab", 8), ("iab", 4), ("acc", 4), ("n24", 24), ("n16", 16), ("trow", 384), ("st", 4),
               ("fac", 144), ("th", 144), ("rk", 4), ("cab", 16), ("cum", 4), ("u2", 4), ("e64", 4), ("pos", 4), ("cw", 16), ("ctw", 32),
               ("ctt", 32), ("ysb", 128)):
    _sb(_n, _w)
_at = 0
for _n, _w in (("bi", 4), ("bib", 4), ("ord", 8), ("emv", 8), ("e32", 32), ("l32", 32), ("m32", 32), ("ta", 32), ("tb", 32), ("s48", 48),
               ("own", 4), ("glf", 4)):
    ALIAS[_n] = ("cs", _at)
    _at += _w
_sb("cs", _at)
for _n, _b, _o in (("bt", "br", 0), ("eye", "br", 96), ("blt", "bp", 0), ("prt", "bp", 128)):
    ALIAS[_n] = (_b, _o)
_sb("pi", 8, "int32")
for _n, _w in (("off", 24), ("gl", 4), ("of2", 8), ("mo", 16), ("ml", 8), ("pl", 16), ("of3", 16)):
    _sb(_n, _w, "uint16")
for _k in range(8):
    SCRATCH["ps%d" % _k] = ("psum", [128, 512], "float32")
SEMAPHORES = ["sv", "ss", "st", "sg", "lx", "lrt", "lgr", "lpr", "lw", "lub", "lv", "axc", "axp", "agc", "agp", "am", "rec", "rep",
              "loc", "o_oc", "o_y", "o_ct", "o_s0", "o_s1", "o_s2", "o_s3"]


def rank_program(g, core, T, topo):
    q = T.rank_of(core)
    if q is None:
        return
    N = len(T.cores)
    eng = {"v": g.vector, "s": g.scalar, "t": g.tensor, "g": g, "y": g.sync}
    own = {"v": "sv", "s": "ss", "t": "st", "g": "sg"}
    total, snaps, log = {}, {}, {}
    seen = {k: {} for k in eng}

    def clash(a, b):
        if a[2] <= b[1] or b[2] <= a[1]:
            return False
        return not (a[3] == b[3] > 1 and (a[1] - b[1]) % a[3])

    def wait(qn, s, v):
        if seen[qn].get(s, 0) >= v:
            return
        eng[qn].wait_ge(T.sem[s], v)
        seen[qn][s] = v
        for k, w in snaps.get((s, v), {}).items():
            seen[qn][k] = max(seen[qn].get(k, 0), w)

    def depend(qn, reads, writes, dma=False):
        need = {}
        for acc, w in [(r, False) for r in reads] + [(r, True) for r in writes]:
            bank = acc[0][:2] == "ps" and len(acc[0]) == 3
            for rec in log.get(acc[0], []):
                if not bank and not clash(acc, rec[0]):
                    continue
                if not (w or rec[1] or (bank and rec[2] != qn)):
                    continue
                if rec[2] == qn and not dma and (not rec[1] or (qn == "t" and bank)):
                    continue
                need[rec[3]] = max(need.get(rec[3], 0), rec[4])
        for s, v in need.items():
            wait(qn, s, v)

    def note(who, reads, writes, s, v):
        for r in writes:
            if r[3] == 1:
                log[r[0]] = [k for k in log.get(r[0], []) if not (r[1] <= k[0][1] and k[0][2] <= r[2])]
        for acc, w in [(r, False) for r in reads] + [(r, True) for r in writes]:
            log.setdefault(acc[0], []).append((acc, w, who, s, v))

    def op(qn, reads, writes, call):
        depend(qn, reads, writes)
        s = own[qn]
        call().then_inc(T.sem[s], 1)
        total[s] = total.get(s, 0) + 1
        snaps[(s, total[s])] = dict(seen[qn])
        note(qn, reads, writes, s, total[s])

    def dma(qn, reads, writes, out, in_, s):
        depend(qn, reads, writes, dma=True)
        eng[qn].dma_start(out, in_).then_inc(T.sem[s], 16)
        total[s] = total.get(s, 0) + 16
        snaps[(s, total[s])] = dict(seen[qn])
        note("dma", reads, writes, s, total[s])

    def R(name, lo, hi, step=1):
        b, o = ALIAS.get(name, (name, 0))
        return (b, lo + o, hi + o, step)

    def ap(r):
        return T[r[0]][:, r[1]:r[2]] if r[3] == 1 else T[r[0]][:, r[1]:r[2]:r[3]]

    def sc_(v):
        return ap(v) if isinstance(v, tuple) else v

    def rds(*vs):
        return [v for v in vs if isinstance(v, tuple)]

    def ts(out, in0, s1, s2, op0, op1=None):
        if op1 is None:
            op("v", rds(in0, s1), [out], lambda: g.vector.tensor_scalar(ap(out), ap(in0), sc_(s1), None, op0))
        else:
            op("v", rds(in0, s1, s2), [out], lambda: g.vector.tensor_scalar(ap(out), ap(in0), sc_(s1), sc_(s2), op0, op1))

    def tt(out, a, b, o, by=None):
        if by is None:
            op("v", [a, b], [out], lambda: g.vector.tensor_tensor(ap(out), ap(a), ap(b), o))
        else:
            op("v", [a, b, by], [out], lambda: g.vector.tensor_tensor(ap(out), ap(a).indirect(ap(by)), ap(b), o))

    def cp(out, a):
        op("v", [a], [out], lambda: g.vector.tensor_copy(ap(out), ap(a)))

    def scatter(win, by, a):
        op("v", [a, by], [win], lambda: g.vector.tensor_copy(ap(win).indirect(ap(by)), ap(a)))

    def ms(out, c):
        op("v", [], [out], lambda: g.vector.memset(ap(out), c))

    def red(out, a, o):
        op("v", [a], [out], lambda: g.vector.tensor_reduce(ap(out), ap(a), AxisListType.X, o))

    def scan(out, a, z, o0, o1, first=-9e29):
        op("v", [a, z], [out], lambda: g.vector.tensor_tensor_scan(ap(out), ap(a), ap(z), first, o0, o1))

    def qz(name, lo, n, tile, t0=0):
        r = R(tile, t0, t0 + 4 * n)
        op("v", [r], [R(name, lo, lo + n), R(name + "_s", lo, lo + n)],
           lambda: g.vector.quantize_mx(T[name][:, lo:lo + n], T[name + "_s"][:, lo:lo + n], ap(r)))

    def act(out, a, f, scale=1.0, bias=0.0, acc=None):
        if acc is None:
            op("s", rds(a, scale, bias), [out], lambda: g.scalar.activation(ap(out), ap(a), f, bias=sc_(bias), scale=sc_(scale)))
        else:
            op("s", rds(a, scale, bias), [out, acc],
               lambda: g.scalar.activation(ap(out), ap(a), f, bias=sc_(bias), scale=sc_(scale), accum_out=ap(acc)))

    def zero(name, lane):
        act(R(name, lane, 512, 4), R("ti", 0, 128), F.Copy, 0.0)

    def mm(bank, lhs, l0, rhs, r0, n, start=True, stop=True):
        op("t", [R(lhs, l0, l0 + 128), R(lhs + "_s", l0, l0 + 128), R(rhs, r0, r0 + n), R(rhs + "_s", r0, r0 + n)], [R(bank, 0, n)],
           lambda: g.tensor.matmul_mx(T[bank][:, 0:n], T[lhs][:, l0:l0 + 128], T[lhs + "_s"][:, l0:l0 + 128],
                                      T[rhs][:, r0:r0 + n], T[rhs + "_s"][:, r0:r0 + n], start, stop))

    def pickc(out, o0, n, win, w0, w1, off, f0):
        fr = R(off, f0, f0 + n // 16)
        op("v", [R(win, w0, w1), fr], [R(out, o0, o0 + n)],
           lambda: g.vector.tensor_copy(T[out][:, o0:o0 + n].bitcast(dt.uint32), T[win][:, w0:w1].bitcast(dt.uint32).indirect(ap(fr))))

    def picks(out, o0, n, win, w0, w1, off, f0):
        fr = R(off, f0, f0 + n // 16)
        op("s", [R(win + "_s", w0, w1), fr], [R(out + "_s", o0, o0 + n)],
           lambda: g.scalar.activation(T[out + "_s"][:, o0:o0 + n], T[win + "_s"][:, w0:w1].indirect(ap(fr)), F.Copy))

    def pick(*a):
        pickc(*a)
        picks(*a)

    def iota(name, n, pattern, cm=0, base=0):
        r = R(name, 0, n)
        op("g", [], [r], lambda: g.iota(ap(r), pattern, base, cm, allow_small_or_imprecise_dtypes=True))

    peers = [c for c in T.cores if c != core]
    far = [c for c in peers if topo.die(c) != topo.die(core)]
    mine = [c for c in T.cores if c not in far]
    near = [mine[(mine.index(core) + j) % len(mine)] for j in range(1, len(mine))]
    bits = lambda es: sum(1 << e for e in es)
    count = lambda m: bin(m).count("1")
    ident = lambda c: DstId(rid=topo.addr(c)[0], pnc=topo.addr(c)[1])

    def lanes(side, turn):
        use = {c: bits(topo.engines(core, c)[side::2][2 * j:2 * j + 2]) for j, c in enumerate(far)}
        es = topo.engines(core, near[0])[1 - side::2]
        es = es[4 * turn:] + es[:4 * turn]
        use[near[0]], use[near[1]], use[near[2]] = bits(es[0:4]), bits(es[4:6]), bits(es[6:8])
        return use

    place = lambda c, at: [k for k in T.cores if k != at].index(c)

    def send(src, start, width, dst, d0, s, to, use):
        blocks = [R(src, start(c), start(c) + width) for c in to]
        depend("g", blocks, [])
        ts_ = []
        for c, r in zip(to, blocks):
            at = d0 + width * place(core, c)
            a, b = ap(r), T[dst][:, at:at + width]
            if SCRATCH[src][2][-2:] == "x4":
                a, b = a.bitcast(dt.uint8), b.bitcast(dt.uint8)
            ts_.append(RemoteDMATransfer(dst_ids=[ident(c)], dma_engine_mask=use[c], remote_sem=T.sem[s], src=a, dst=b))
        g.remote_dma_fused(ts_, local_sem=T.sem["loc"])
        total["loc"] = total.get("loc", 0) + sum(count(use[c]) for c in to)
        note("dma", blocks, [], "loc", total["loc"])

    def arrives(dst, d0, width, s):
        total[s] = sum(count(m) for m in lanes(0, 0).values())
        note("dma", [], [R(dst, d0, d0 + width * len(peers))], s, total[s])

    def load(qn, name, w, src, s, at=0):
        r = R(name, at, at + w)
        dma(qn, [], [r], ap(r), src, s)

    load("y", "xt", 512, T.x[:, :], "lx")
    load("s", "xt", 32, T.rt[:, 0:32], "lrt", 544)
    load("y", "gt", 512, T.gr[:, :], "lgr")
    load("s", "pb", 4, T.pr[:, 0:4], "lpr")
    load("y", "wb", 2048, T.w[:, :], "lw")
    load("s", "ubb", 2048, T.ub[:, :], "lub")
    load("y", "bv", 512, T.v[:, :], "lv", 64)

    iota("pi", 1, [[1, 1]], cm=1)
    iota("ti", 144, [[1, 144]])
    iota("rp", 128, [[0, 8], [1, 16]])
    iota("bi", 3, [[16, 3]])
    iota("e128", 128, [[1, 8], [0, 16]])
    iota("e32", 32, [[1, 8], [0, 4]])
    iota("l32", 32, [[0, 8], [1, 4]])
    iota("s48", 48, [[1, 3], [3, 16]])
    iota("glf", 3, [[128, 3]], cm=1)
    col = lambda k: R("sc", k, k + 1)
    pF, iF, eF, iH, e16, negi, i4, i3 = [col(k) for k in range(8)]
    TI, RP, E128 = R("ti", 0, 128), R("rp", 0, 128), R("e128", 0, 128)
    p0 = R("pi", 0, 1)
    ms(R("xt", 512, 544), 0.0)
    ms(R("pm", 0, 40), FLOOR)
    ms(R("gt", 512, 544), 0.0)
    ts(R("pi", 1, 2), p0, 15, None, A.bitwise_and)
    ts(R("pi", 2, 3), p0, 4, None, A.arith_shift_right)
    ms(R("br", 0, 616), 0.0)
    cp(R("sc", 0, 3), R("pi", 0, 3))
    ms(R("bv", 0, 64), 0.0)
    ms(R("ctw", 0, 32), 0.0)
    ts(R("eye", 4, 516, 4), TI, pF, None, A.is_equal)
    for lane in (0, 1):
        ts(R("tri", lane, 512, 4), TI, pF, None, A.is_ge)
    for lane in (2, 3):
        ts(R("tri", lane, 512, 4), RP, iF, None, A.is_equal)
    zero("tk", 2)
    zero("tk", 3)
    act(iH, iF, F.Identity, 1.0, 0.5)
    act(R("bib", 0, 3), R("bi", 0, 3), F.Identity, 1.0, iH)
    order = [T.rank_of(c) for c in [core] + sorted(near) + far]
    m = 0
    while m < N:
        n = 1
        while m + n < N and order[m + n] == order[m] + n:
            n += 1
        act(R("ord", m, m + n), R("ti", order[m], order[m] + n), F.Copy)
        m += n
    zero("at", 3)
    qz("xq", 0, 144, "xt")
    mm("ps0", "xq", 0, "xq", 16, 128)
    qz("xq", 144, 128, "tri")
    qz("ebq", 0, 128, "eye", 4)

    S = R("ps0", 120, 128)
    scan(R("pm", 1, 9), S, R("pm", 32, 40), A.max, A.max)
    ts(R("emv", 0, 8), R("ord", 0, 8), eF, None, A.is_equal)
    act(R("junk", 0, 8), R("pm", 1, 9), F.Sign, -1.0, R("pm", 8, 9), R("iab", 0, 1))
    ts(R("cm", 0, 8), R("pm", 1, 9), R("pm", 8, 9), BIG, A.is_lt, A.mult)
    ts(R("m32", 0, 32), R("e32", 0, 32), eF, None, A.is_equal)
    tt(R("ab", 0, 8), R("cm", 0, 8), R("pm", 0, 8), A.add)
    ts(R("nz", 0, 128), RP, 0.5, None, A.is_gt)
    scan(R("pm", 17, 25), S, R("ab", 0, 8), A.max, A.min)
    act(R("junk", 8, 16), R("pm", 17, 25), F.Sign, -1.0, R("pm", 24, 25), R("iab", 1, 2))
    ts(R("tk", 0, 512, 4), E128, R("iab", 0, 1), None, A.is_equal)
    qz("ebq", 128, 128, "eye", 3)
    ts(R("tk", 1, 512, 4), E128, R("iab", 1, 2), None, A.is_equal)
    cp(R("gl", 0, 3), R("glf", 0, 3))
    qz("xq", 288, 128, "tk")

    mm("ps1", "xq", 288, "xq", 142, 130)
    mm("ps2", "xq", 288, "xq", 142, 130)
    qz("xq", 416, 136, "gt")
    qz("ebq", 256, 128, "eye", 2)
    for k in range(2):
        act(R("junk", 16 + 128 * k, 144 + 128 * k), R("ps1", 2, 130), F.Sign, -1.0, R("bib", k, k + 1), R("acc", k, k + 1))
    ts(R("tmpc", 0, 128), R("ps2", 2, 130), R("bib", 2, 3), 0.5, A.is_lt, A.subtract)
    act(e16, eF, F.Identity, 16.0, -128.0)
    red(R("acc", 2, 3), R("tmpc", 0, 128), A.add)
    mm("ps3", "xq", 144, "xq", 288, 130)
    for k in range(2):
        act(R("n24", k, 24, 3), R("emv", 0, 8), F.Copy, R("acc", k, k + 1))
    ts(R("n24", 2, 24, 3), R("emv", 0, 8), R("acc", 2, 3), 2.0, A.mult, A.mult)
    tt(R("cab", 0, 8), R("ps3", 0, 128, 16), R("tk", 0, 512, 64), A.mult)
    ts(R("bt", 2, 96, 4), R("n24", 0, 24), MAGIC16, MAGIC16, A.add, A.subtract)
    tt(R("cab", 8, 16), R("ps3", 0, 128, 16), R("tk", 1, 512, 64), A.mult)
    tt(R("bt", 3, 96, 4), R("n24", 0, 24), R("bt", 2, 96, 4), A.subtract)
    red(R("cum", 0, 1), R("cab", 0, 8), A.add)
    qz("xq", 552, 128, "bt")
    mm("ps4", "xq", 144, "xq", 542, 128)
    red(R("cum", 1, 2), R("cab", 8, 16), A.add)
    qz("ebq", 384, 128, "eye", 1)
    ts(R("off", 0, 24), R("ps4", 10, 34), 0.5, 64.0, A.mult, A.add)
    act(negi, iF, F.Copy, -1.0)
    act(i4, iF, F.Copy, 4.0)
    act(i3, iF, F.Copy, 3.0)
    act(R("e64", 0, 2), R("iab", 0, 2), F.Copy, 64.0)
    ts(R("u2", 0, 2), R("cum", 0, 2), 49.0, -257.0, A.min, A.add)

    out = lambda c: 336 + 48 * order.index(T.rank_of(c))
    pick("lx", 528, 192, "xq", 0, 144, "off", 12)
    pick("lx", 336, 192, "xq", 0, 144, "off", 0)
    pick("lg", 336, 384, "xq", 416, 552, "off", 0)
    send("lx", out, 48, "lx", 0, "axc", far, lanes(0, 0))
    send("lx", out, 48, "lx", 0, "axc", near, lanes(0, 0))
    send("lx_s", out, 48, "lx_s", 0, "axp", peers, lanes(1, 0))
    send("lg", out, 48, "lg", 0, "agc", peers, lanes(1, 1))
    send("lg_s", out, 48, "lg_s", 0, "agp", peers, lanes(0, 1))
    for name, s in (("lx", "axc"), ("lx_s", "axp"), ("lg", "agc"), ("lg_s", "agp")):
        arrives(name, 0, 48, s)

    iota("rw", 512, [[0, 512]], base=144)
    qz("wq", 0, 512, "wb")
    tt(R("pos", 0, 2), R("u2", 0, 2), R("e64", 0, 2), A.add)
    for k in range(2):
        act(R("n16", 8 * k, 8 * k + 8), R("m32", 0, 32, 4), F.Copy, R("pos", k, k + 1))
    act(R("ta", 0, 32), R("l32", 0, 32), F.Identity, 128.0, e16)
    act(R("tb", 0, 32), R("l32", 0, 32), F.Identity, 1.0, negi)
    act(R("own", 0, 3), R("ti", 0, 3), F.Identity, 1.0, i3)
    act(R("blt", 32, 64), R("m32", 0, 32), F.Copy, i4)
    act(R("blt", 64, 96), R("m32", 0, 32), F.Copy, iF)
    for lane in range(4):
        act(R("prt", lane, 512, 4), TI, F.Identity, 0.0, R("pb", lane, lane + 1))
    qz("rl", 240, 144, "bv")
    ts(R("bt", 2, 64, 4), R("n16", 0, 16), MAGIC16, MAGIC16, A.add, A.subtract)
    tt(R("blt", 0, 32), R("ta", 0, 32), R("m32", 0, 32), A.mult)
    tt(R("bt", 3, 64, 4), R("n16", 0, 16), R("bt", 2, 64, 4), A.subtract)
    tt(R("blt", 96, 128), R("tb", 0, 32), R("m32", 0, 32), A.mult)
    qz("xq", 552, 128, "bt")
    mm("ps4", "xq", 144, "xq", 542, 128)
    for k in range(3):
        ts(R("fac", 48 * k, 48 * k + 48), R("s48", 0, 48), R("own", k, k + 1), BELOW, A.is_ge, A.max)
    ts(R("pl", 0, 16), R("ps4", 10, 26), 256.0, None, A.add)
    qz("uq", 0, 512, "ubb")
    qz("bq", 0, 160, "bp")

    MK = lambda b: R("mk", 384 * b, 384 * b + 384)
    for i in range(4):
        mm("ps%d" % i, "wq", 128 * i, "lx", 0, 384)
    act(R("sg", 0, 384), R("ps0", 0, 384), F.Sign)
    act(MK(0), R("sg", 0, 384), F.Relu)
    for b in (1, 2, 3):
        ts(MK(b), R("ps%d" % b, 0, 384), 0.0, None, A.is_gt)
    for b in range(4):
        mm("ps%d" % (4 + b), "ebq", 128 * b, "lg", 0, 384)

    def masked(k, b):
        tt(R("mt", 512 * k + b, 512 * k + 512, 4), R("ps%d" % (4 + b), k, 384, 3), R("mk", 384 * b + k, 384 * b + 384, 3), A.mult)

    for b in range(4):
        masked(0, b)
        masked(1, b)
    masked(2, 0)
    qz("mq", 0, 256, "mt")
    for b in (1, 2, 3):
        masked(2, b)
    qz("mq", 256, 128, "mt", 1024)

    parts = ((0, 256), (256, 128))
    UB = (("ps3", "ps0", "ps1", "ps2"), ("ps6", "ps7", "ps4", "ps5"))

    def product(h, i):
        mm(UB[h][i], "uq", 128 * i, "mq", parts[h][0], parts[h][1])

    def shrink(qn, h, i):
        o, n = parts[h]
        if qn == "s":
            act(R("dxt", 4 * o + i, 4 * (o + n), 4), R(UB[h][i], 0, n), F.Copy, 0.0625)
        else:
            ts(R("dxt", 4 * o + i, 4 * (o + n), 4), R(UB[h][i], 0, n), 0.0625, None, A.mult)

    st = lambda k: R("st", k, k + 1)
    w48 = lambda name, k: R(name, 48 * k, 48 * k + 48)
    for k in (0, 1):
        mm("ps%d" % k, "mq", 128 * k, "bq", 32, 128)
    mm("ps2", "bq", 32, "mq", 0, 256)
    product(0, 0)
    for k in (0, 1):
        act(st(k), R("ps%d" % k, 0, 1), F.Abs, 1.0, TINY)
    act(R("trow", 0, 256), R("ps2", 0, 256), F.Abs, 1.0, TINY)
    product(0, 1)
    product(0, 2)
    mm("ps4", "bq", 32, "mq", 256, 128)
    mm("ps5", "mq", 256, "bq", 32, 128)
    product(0, 3)
    for k in (0, 1):
        act(w48("th", k), w48("fac", k), F.Copy, st(k))
    act(R("trow", 256, 384), R("ps4", 0, 128), F.Abs, 1.0, TINY)
    act(st(2), R("ps5", 0, 1), F.Abs, 1.0, TINY)
    act(w48("th", 2), w48("fac", 2), F.Copy, st(2))
    for i in range(4):
        product(1, i)
    shrink("v", 0, 0)
    shrink("v", 0, 1)
    shrink("s", 0, 2)
    shrink("s", 0, 3)
    for k in range(3):
        tt(w48("cmp", k), R("trow", 0, 384), w48("th", k), A.is_gt, R("gl", 0, 3))
    for k in range(3):
        red(R("rk", k, k + 1), w48("cmp", k), A.add)
    for k in range(3):
        ts(R("at", k, 512, 4), RP, R("rk", k, k + 1), None, A.is_equal)
    qz("atq", 0, 128, "at")
    mm("ps3", "atq", 0, "bq", 0, 128, True, False)
    mm("ps3", "atq", 0, "bq", 16, 128, False, True)
    for i in range(4):
        shrink("s", 1, i)
    qz("dxw", 0, 256, "dxt")
    ts(R("mo", 0, 16, 2), R("ps3", 8, 16), 64.0 * q, None, A.add)
    ts(R("of2", 0, 8), R("ps3", 0, 8), 128.0, None, A.add)
    qz("dxw", 256, 128, "dxt", 1024)
    pick("rl", 0, 128, "dxw", 0, 384, "of2", 0)

    send("mo", lambda c: 2 * place(c, core), 1, "ml", 0, "am", peers, lanes(0, 0))
    send("rl", lambda c: 16 * place(c, core), 16, "rl", 128, "rec", peers, lanes(1, 0))
    send("rl_s", lambda c: 16 * place(c, core), 16, "rl_s", 128, "rep", peers, lanes(0, 1))
    arrives("ml", 0, 1, "am")
    arrives("rl", 128, 16, "rec")
    arrives("rl_s", 128, 16, "rep")

    RW = R("rw", 0, 512)
    h128 = lambda name, h: R(name, 128 * h, 128 * h + 128)
    ends = lambda h: R("gs", 128 * h + 15, 128 * h + 128, 16)
    scatter(RW, R("mo", 14, 15), R("ti", 16, 32))
    scatter(RW, R("ml", 0, 7), R("ti", 32, 144))
    for h in range(2):
        tt(h128("gm", h), RW, R("tri", 2, 512, 4), A.mult, R("pl", 8 * h, 8 * h + 8))
    for h in range(2):
        scan(h128("gs", h), R("nz", 0, 128), h128("gm", h), A.mult, A.add, 0.0)
    for h in range(2):
        cp(R("of3", 8 * h, 8 * h + 8), ends(h))

    for h in range(2):
        pick("zc", 128 * h, 128, "rl", 96, 256, "of3", 8 * h)
        for b in range(4):
            mm("ps%d" % (4 + b), "ebq", 128 * b, "zc", 128 * h, 128, h == 0, h == 1)
    for h in range(2):
        ts(R("cw", 8 * h, 8 * h + 8), ends(h), 143.5, 1.0 + h, A.is_lt, A.mult)
    tt(R("ctw", 0, 8), R("cw", 0, 8), R("cw", 8, 16), A.add)
    op("v", [R("ctw", 0, 32)], [R("ctt", 0, 32)], lambda: g.vector.transpose(T.ctt[0:32, 0:32], T.ctw[0:32, 0:32]))
    dma("y", [R("ctt", 0, 32)], [], T.ct[:, :], T.ctt[0:8, 0:16], "o_ct")
    for b in (0, 2):
        act(R("zt", b, 512, 4), R("ps%d" % (4 + b), 0, 128), F.Copy)
    for b in (1, 3):
        cp(R("zt", b, 512, 4), R("ps%d" % (4 + b), 0, 128))
    qz("zq", 0, 128, "zt")
    mm("ps3", "rl", 256, "zq", 0, 128)
    dma("y", [R("zq", 0, 128)], [], T.oc[:, :], T.zq[:, 0:128].bitcast(dt.uint8), "o_oc")
    for k in range(4):
        dma("y" if k < 1 else "s", [R("zq_s", 0, 128)], [], T.osc[4 * k:4 * k + 4, 0:128], T.zq_s[32 * k:32 * k + 4, 0:128], "o_s%d" % k)
    cp(R("ysb", 0, 128), R("ps3", 0, 128))
    dma("y", [R("ysb", 0, 128)], [], T.y[:, :], T.ysb[:, 0:128], "o_y")

    for s, v in total.items():
        wait("g", s, v)
